import numpy as np, ml_dtypes
CORES = [3,7,11,15,131,135,139,143]
N = 8
import mx_ref
BF = ml_dtypes.bfloat16
def tile(rs):
    return np.stack(rs, axis=2).reshape(128, -1).astype(BF)
def pick(q, e):
    c = np.concatenate([q[0].reshape(128, -1, 4), np.zeros((128, 1, 4), np.uint8)], axis=1); s = np.concatenate([q[1], np.ones((16, 1), np.uint8)], axis=1)
    return (np.ascontiguousarray(c[:, e].reshape(128, -1)), np.ascontiguousarray(s[:, e]))
def join(*qs):
    return (np.concatenate([q[0] for q in qs], axis=1), np.concatenate([q[1] for q in qs], axis=1))
def put(q, e, v):
    c, s = q[0].reshape(128, -1, 4).copy(), q[1].copy(); c[:, e] = v[0].reshape(128, -1, 4); s[:, e] = v[1]
    return (c.reshape(128, -1), s)
def pk(c, s):
    return (np.ascontiguousarray(c), mx_ref.live(s))
def emit(q):
    return q[0], q[1]
def packed(v, rng):
    q = [mx_ref.quantize(np.ascontiguousarray(v[r])) for r in range(N)]
    return np.stack([a for a, b in q]), np.stack([mx_ref.plane(b, rng) for a, b in q])
def values_of_codes():
    e, c = np.zeros((128, 128, 4), np.float32), np.zeros((128, 2, 4), np.uint8)
    e[np.arange(128), np.arange(128), 0] = 1
    c[:127, :, 0] = np.arange(256).reshape(2, 128).T[:127]
    return mx_ref.matmul(mx_ref.quantize(e.reshape(128, 512).astype(BF)), (c.reshape(128, 8), np.full((16, 2), 127, np.uint8))).T.reshape(-1).astype(np.float64)
CODE_VALUE, SCALE_VALUE = values_of_codes(), 2.0 ** (np.arange(256) - 127.0)
def decode(q):
    return (CODE_VALUE[q[0]].reshape(16, 8, -1, 4) * SCALE_VALUE[q[1]][:, None, :, None] + 0.0).reshape(128, -1).astype(np.float32)
def f(rng, *shape):
    return mx_ref.flush((rng.standard_normal(shape, dtype=np.float32) * np.exp2(rng.integers(-2, 3, shape[:-1] + (1,)))).astype(BF))
def wide(rng, *shape, cols=0):
    v = rng.standard_normal(shape, dtype=np.float32) * np.exp2(rng.integers(-12, 13, shape)).astype(np.float32)
    if cols: v *= np.repeat(np.exp2(rng.integers(-cols, cols + 1, shape[:-2] + (1, shape[-1] // 4))) * (rng.random(shape[:-2] + (1, shape[-1] // 4)) > 0.0625), 4, axis=-1).astype(np.float32)
    return mx_ref.flush(v.astype(BF))
C, H = 288, 144
MASK = [4, 1, 2]
def numbers_of(rng):
    return {"x": np.array(f(rng, N, 128, 4 * C)), "u": np.array(f(rng, N, 128, 512)), "v": np.array(f(rng, N, 128, 512))}
def weights(rng, w):
    c, s = packed(np.ascontiguousarray(w).reshape(N, 128, 2048), rng)
    return {"wc": c, "ws": s}
def layers(rng, still=[], pairs=False):
    w = np.array(f(rng, N, 128, 2048)).reshape(N, 8, 16, 4, 8, 16, 4)
    for i in still:
        w[:, :, i] = 0
        w[:, :, :, :, :, i] = 0
    if pairs:
        w[:, :, :, :, :, 8:] = 0
        for g in range(8):
            w[:, g, 8, 0, g, 8, 0] = -28.0
            for b in range(4): w[:, g, 10, b, g, 9, 0] = -2.0 ** (b - 5)
    return weights(rng, w)
def setup_inputs(rng):
    return {**numbers_of(rng), **layers(rng)}
def setup_inputs_ties(rng):
    d = numbers_of(rng)
    o = rng.permutation(N)
    k = rng.integers(0, 4, (N, 8, C))
    k[o[1]] += 1
    k[o[2], rng.permutation(8)[:4]] = 1
    for g in range(8): k[o[3], g] = 1 + (rng.permutation(C) < H + g % 3 - 1)
    x = d["x"].reshape(N, 8, 16, C, 4)
    x[:, :, 0] = 0
    x[:, :, 0, :, 0] = k.astype(np.float32).astype(BF)
    a = np.exp2(rng.integers(-3, 4, (N, 8, C)).astype(np.float32))
    x[:, :, 8:] = 0
    x[:, :, 8, :, 0] = (-1.125 * a).astype(BF)
    x[:, :, 10, :, 0] = (-0.0703125 * a).astype(BF)
    u = d["u"].reshape(N, 128, 128, 4)
    u[:, :, ::16] = 0
    for r in range(N):
        for h in range(0, 128, 16): u[r, h, h, 0] = 0.0 if r == o[0] else -1.0 if r == o[1] else 1.0
    return {"x": x.reshape(N, 128, 4 * C), "u": u.reshape(N, 128, 512), "v": d["v"], **layers(rng, [0], True)}
def setup_inputs_near(rng):
    d = numbers_of(rng)
    x = d["x"].astype(np.float32).reshape(N, 8, 16, C, 4)
    x[:, :, 0] = 0
    x[:, :, 8:] = 0
    u = d["u"].reshape(N, 128, 128, 4)
    u[:, :, ::16] = 0
    o = rng.permutation(N) % 4
    for r in range(N):
        c = rng.choice([-1.0, 1.0], (8, 1))
        s = rng.integers(0, 16, (8, C))
        digits = ((s[:, :, None] >> np.arange(4)) & 1) * np.exp2(np.arange(4) - 23.0)
        if o[r] < 2:
            x[r, :, 0, :, 0] = c
            x[r, :, 8] = digits
            x[r, :, 11, :, 0] = 2.0 ** -10
        elif o[r] == 2: x[r, :, 8] = digits * rng.choice([-1.0, 1.0], (8, C, 1))
        else:
            x[r, :, 8, :, 0] = np.where(s < 8, 1.25, 0.0) * 2.0 ** -30 * c
            x[r, :, 9, :, 0] = np.where(s < 8, 0.0, 1.125) * 2.0 ** -30 * c
            for g in rng.permutation(8)[:4]:
                e = rng.choice([-1.0, 1.0], C) * 2.0 ** -30
                x[r, g, 8, :, 0] = 1.25 * e
                x[r, g, 9, :, 0] = -1.125 * e
        at = [0, C - 1, int(rng.integers(C)), int(rng.integers(C))]
        for g, j in zip(rng.permutation(8)[:4], at): x[r, g, 0, j, 0] = 2.0 ** 29 * rng.choice([-1.0, 1.0])
        k = 1.0 if o[r] == 0 else 2.0 ** -30
        for h in range(0, 128, 16):
            u[r, h, h, 0] = k if o[r] < 2 else 1.0
            if o[r] < 2: u[r, h + 11, h, 0] = k
            if o[r] < 3: u[r, h + 8, h] = k
            else:
                u[r, h + 8, h, 0] = k
                u[r, h + 9, h, 0] = 1.125 * k
    return {"x": x.reshape(N, 128, 4 * C).astype(BF), "u": u.reshape(N, 128, 512), "v": d["v"], **layers(rng, [0, 8, 9, 10, 11, 12, 13, 14, 15])}
def setup_inputs_odd(rng):
    d = numbers_of(rng)
    o = rng.permutation(N)
    x = (1.0 + (2 * rng.integers(0, 64, (N, 16, 8, C, 4)) + 1) * 2.0 ** -7) * np.exp2(-rng.integers(0, 7, (N, 16, 8, C, 4)).astype(np.float64)) * rng.choice([-1.0, 1.0], (N, 16, 8, C, 4))
    s = rng.choice([-1.0, 1.0], (N, 8, 2, C))
    late = np.arange(C) >= H
    e = np.arange(C)[None, :] - np.where(np.arange(8)[:, None] < rng.integers(1, 8), 1, 0)
    s[o[0], :, 0] = np.where(late, 1.0, -1.0)
    s[o[1], :, 0] = np.where((e >= 0) & (e < H), 1.0, -1.0)
    s[o[2], :, 0] = np.where(late[None, :] == (rng.permutation(8)[:, None] < 4), 1.0, -1.0)
    x[:, :, 0, :, 0] = 1.96875 * 2.0 ** 8 * s.reshape(N, 16, C)
    u = d["u"].reshape(N, 16, 8, 128, 4)
    u[:, :, 0, ::16] = 0
    for r in o[:3]:
        u[r, :, :, ::16] = 0
        for g in range(8): u[r, 2 * g, 0, 16 * g, 0] = 1.0
    for i, g in enumerate(rng.permutation(8)[:4]):
        x[o[3], 2 * g, 1, :, 0] = (8 + rng.integers(0, 2, C)) * 2.0 ** (i - 8)
        u[o[3], :, :, 16 * g] = 0
        u[o[3], 2 * g, 1, 16 * g, 0] = 1.0
    return {"x": x.astype(np.float32).reshape(N, 128, 4 * C).astype(BF), "u": u.reshape(N, 128, 512), "v": d["v"], **layers(rng, [0, 8])}
def setup_inputs_ends(rng):
    d = numbers_of(rng)
    x = np.zeros((N, 8, 16, C, 4))
    u = d["u"].astype(np.float32).reshape(N, 128, 128, 4)
    v = d["v"].astype(np.float32)
    w = np.zeros((N, 128, 4, 128, 4), np.float32)
    o = rng.permutation(N) % 4
    i = np.arange(128)
    for r in range(N):
        h = rng.permutation(8)
        c = np.where(h < 2, 0.0, h % 2 * 2.0 - 1.0)[None, :, None]
        low = -(0.9 + 0.1 * rng.random((8, 16, C, 4))) * 2.0 ** 30
        if o[r] == 0: x[r] = low
        if o[r] == 1: x[r] = np.where((rng.random(C) < 0.5)[:, None], (1.0 + 0.4 * rng.random((8, 16, C, 4))) * 2.0 ** 27, low)
        if o[r] == 2: x[r] = -(1.0 + 0.125 * rng.integers(0, 8, (8, 16, C, 4))) * 2.0 ** -30
        if o[r] == 3: x[r] = d["x"][r].astype(np.float32).reshape(8, 16, C, 4)[:, :, :1]
        if o[r] < 2:
            u[r, :, ::16] = c * (0.9 + 0.1 * rng.random((128, 8, 4))) * 2.0 ** 30
            v[r] = rng.choice([-1.0, 1.0], (128, 512)) * (0.9 + 0.1 * rng.random((128, 512))) * 2.0 ** 30
        if o[r] == 2:
            u[r, :, ::16] = c * (1.0 + 0.125 * rng.integers(0, 8, (128, 8, 4))) * 2.0 ** -30
            v[r] = rng.choice([-1.0, 1.0], (128, 512)) * (1.0 + 0.125 * rng.integers(0, 8, (128, 512))) * 2.0 ** -30
        if o[r] == 3: u[r, :, ::16] *= np.abs(c).astype(np.float32)
        k = np.array([4.0, 8.0, 16.0])[rng.permutation(8) % 3]
        for b in range(4): w[r, i, b, i, b] = k[i // 16]
    return {"x": x.astype(np.float32).reshape(N, 128, 4 * C).astype(BF), "u": u.reshape(N, 128, 512).astype(BF), "v": v.astype(BF), **weights(rng, w.astype(BF))}
def setup_inputs_spread(rng):
    d = setup_inputs(rng)
    d["x"] = wide(rng, N, 128, 4 * C, cols=6)
    return d
def check_inputs(d):
    b = []
    for k in ("x", "u", "v"):
        a = np.abs(d[k].astype(np.float32))
        if not (np.isfinite(a).all() and ((a == 0) | (a >= 2.0 ** -30) & (a <= 2.0 ** 30)).all()): b.append("a value of " + k)
    none, least, most = [emit(mx_ref.quantize(np.full((128, 16), k, np.float32).astype(BF)))[1][0, 0] for k in (0.0, 2.0 ** -8, 2.0 ** 8)]
    for r in range(N):
        if ((d["wc"][r] == 0x7F) | (d["wc"][r] == 0xFF)).any(): b.append("wc: a code that is no number")
        s = mx_ref.live(d["ws"][r])
        if ((s != none) & ((s < least) | (s > most))).any(): b.append("ws: a scale out of range")
    return b
def parts(t):
    return np.ascontiguousarray(t.reshape(8, 16, -1, 4).transpose(2, 0, 1, 3)).reshape(-1, 16, 4)
def laid(p):
    return np.ascontiguousarray(p.reshape(-1, 8, 16, 4).transpose(1, 2, 0, 3)).reshape(128, -1)
def layer(w, q):
    return mx_ref.quantize(tile([np.maximum(mx_ref.matmul(pick(w, np.arange(128 * b, 128 * b + 128)), q), np.float32(0.0)) * np.float32(0.03125) for b in range(4)]))
def reference(x, u, v, wc, ws):
    qu = [mx_ref.quantize(u[r]) for r in range(N)]
    lay = [pk(wc[r], ws[r]) for r in range(N)]
    now = [x[r] for r in range(N)]
    for m in MASK:
        t, high, low, own, out = [], [], [], [], []
        for r in range(N):
            q = mx_ref.quantize(now[r])
            s = mx_ref.matmul(qu[r], q)[::16] + np.float32(0.0)
            flag = np.zeros((8, C), bool)
            np.put_along_axis(flag, np.argsort(-s, axis=1, kind="stable")[:, :H], True, axis=1)
            high.append(np.flatnonzero(flag.T))
            low.append(np.flatnonzero(~flag.T))
            t.append(decode(q))
            p = parts(t[r].astype(BF))
            own.append(mx_ref.quantize(laid(p[high[r]])))
            out.append(mx_ref.quantize(laid(p[low[r]])))
        home = [layer(lay[r], own[r]) for r in range(N)]
        guest = [layer(lay[r], out[r ^ m]) for r in range(N)]
        for r in range(N):
            a = np.zeros((8 * C, 16, 4), np.float32)
            a[high[r]] = parts(decode(home[r]))
            a[low[r]] = parts(decode(guest[r ^ m]))
            now[r] = (t[r] + laid(a)).astype(BF)
    y, op = np.zeros((N, 128, C), np.float32), np.zeros((N, 8, C), np.float32)
    oc, osc = np.zeros((N, 128, 4 * C), np.uint8), np.zeros((N, 16, C), np.uint8)
    for r in range(N):
        q = mx_ref.quantize(now[r])
        y[r] = mx_ref.matmul(mx_ref.quantize(v[r]), q)
        n = np.zeros(8 * C, np.int64)
        n[high[r]] = np.arange(4 * C)
        n[low[r]] = 4 * C + np.arange(4 * C)
        op[r] = n.reshape(C, 8).T
        oc[r], osc[r] = emit(q)
    return {"y": y, "op": op, "oc": oc, "osc": osc}

@@ -1,0 +1,406 @@
+from concourse.mybir import dt, AluOpType, AxisListType, ActivationFunctionType
+
+MASK = [4, 1, 2]
+C, H = 288, 144
+NV = 8
+TB = 1160
+F8, U8, BF, F32, I32, U16 = "float8_e4m3fn_x4", "uint8", "bfloat16", "float32", "int32", "uint16"
+
+SCRATCH = {}
+_SHARE = {}
+
+
+def _add(dtype, *sizes):
+    for n, w in sizes:
+        SCRATCH[n] = ("sbuf", [128, w], dtype)
+
+
+def _mx(*sizes):
+    for n, w in sizes:
+        SCRATCH[n] = ("sbuf", [128, w], F8)
+        SCRATCH[n + "s"] = ("sbuf", [128, w], U8)
+
+
+def _pack(into, dtype, *sizes):
+    at = 0
+    for n, w in sizes:
+        _SHARE[n] = (into, at, w)
+        at += (w + 7) // 8 * 8
+    SCRATCH[into] = ("sbuf", [128, at], dtype)
+
+
+_mx(("q", C), ("uq", 128), ("urq", 128), ("vq", 128), ("wq", 512), ("gq", H), ("fq", H), ("aq", H), ("bq", H), ("nq", 128),
+    ("scq", 704), ("f2q", C), ("gaq", 128), ("gbq", 128), ("s1q", 128), ("s2q", 128), ("s3q", 128), ("s4q", 128), ("lzq", 240))
+_mx(*[("flq%d" % k, C) for k in range(5)], *[("idq%d" % k, 256) for k in range(4)])
+_mx(*[("%s%d" % (n, k), H) for n in ("lg", "lb") for k in range(3)])
+_add(BF, *[("fl%d" % k, 4 * C) for k in range(5)])
+_add(BF, ("xt", 4 * C), ("ut", 512), ("vt", 512), ("gt", 4 * H), ("ft", 4 * H), ("at", 4 * H), ("bt", 4 * H), ("tw", 8 * TB),
+     ("vw", 8 * 4 * C), ("scw", 2816), ("fe", 512), ("fe2", 4 * C), ("wk", 1032), ("val", C), ("junk", C))
+_pack("ctile", BF, ("cga", 512), ("cgb", 512), ("cs1", 512), ("cs2", 512), ("cs3", 512), ("cs4", 512), ("clz", 960))
+_pack("rows", F32, ("zf", C), ("r256", 256), ("r18", C), ("rg4", 512), ("rr", 128), ("rv", C), ("rs", 72), ("rt", 72), ("ry", 72),
+      ("r4c", 18), ("rp", C))
+_pack("cons", F32, ("cf", 8), ("cx", 32), ("mo", C), ("mv", C), ("ms", 72), ("nc", 72), ("yc", 72), ("pc", C))
+_pack("temp", F32, ("mm", C), ("f1", 144), ("f2", 72), ("f3", 36), ("n1", C), ("m1", C), ("ec", C), ("hs", C), ("key", C),
+      ("sm", 32), ("cc", 72), ("xx", 72), ("zz", 72), ("t2", 72), ("nn", 72), ("ra", 72), ("rb", 72), ("sl0", 72), ("sl1", 36),
+      ("v1", 18), ("w1", 18), ("e1", 18), ("o1", 72), ("o2", 72), ("o3", 72), ("p1", 72), ("p2", 72), ("p3", 72), ("nr", C),
+      ("cr", C), ("xr", C), ("yr", C), ("zr", C))
+_pack("ints", I32, ("ci", 8), ("ru", 8), ("n18", 18), ("h18", 18), ("yi", 72), ("si", 72), ("yn", 72), ("sn", 72), ("ni", 72), ("cn", 72))
+_add(F32, ("own", 24), ("dg", 72), ("yo", C))
+_add(U16, ("ul", 8), ("vl", 18), ("sl", 18), ("off", 72), ("off2", 72))
+SCRATCH["ps"] = ("psum", [128, 4096], F32)
+
+SEMAPHORES = (["qv", "qs", "qp", "qg", "dx", "du", "dv", "dw", "oy", "oo", "oq"]
+              + ["%s%d" % (n, r) for n in ("tr", "ga", "bl", "sg", "sb") for r in range(3)])
+
+
+def rank_program(g, core, T, topo):
+    rank = T.rank_of(core)
+    if rank is None:
+        return
+    A, F, X = AluOpType, ActivationFunctionType, AxisListType
+    queue = {"v": g.vector, "s": g.scalar, "p": g.tensor, "g": g, "y": g.sync}
+    total, seen, last, banks = {}, {}, {}, {}
+
+    def v(name, a=0, b=None, st=1):
+        buf, at, w = _SHARE[name] if name in _SHARE else (name, 0, SCRATCH[name][1][1])
+        b = w if b is None else b
+        return T[buf][:, at + a:at + b] if st == 1 else T[buf][:, at + a:at + b:st]
+
+    def before(q, R, W, B):
+        deps = {}
+        toks = [t for k in R for t in last.get(k, ([], []))[0]]
+        toks += [t for k in W for half in last.get(k, ([], [])) for t in half]
+        toks += [t for b in B for qq, t in banks.get(b, {}).items() if qq != q]
+        for s, n in toks:
+            deps[s] = max(deps.get(s, 0), n)
+        for s, n in deps.items():
+            if seen.get((q, s), 0) < n:
+                queue[q].wait_ge(T.sem[s], n)
+                seen[(q, s)] = n
+
+    def after(q, R, W, B, tok):
+        for k in R:
+            last.setdefault(k, ([], []))[1].append(tok)
+        for k in W:
+            last[k] = ([tok], [])
+        for b in B:
+            banks.setdefault(b, {})[q] = tok
+
+    def op(q, call, R=(), W=(), B=()):
+        before(q, R, W, B)
+        s = "q" + q
+        call().then_inc(T.sem[s], 1)
+        total[s] = total.get(s, 0) + 1
+        after(q, R, W, B, (s, total[s]))
+
+    def dma(q, s, pairs, R=(), W=()):
+        before(q, R, W, ())
+        for o, i in pairs:
+            queue[q].dma_start(o, i).then_inc(T.sem[s], 16)
+            total[s] = total.get(s, 0) + 16
+        after(q, R, W, (), (s, total[s]))
+
+    def ts(o, i, s1, o1, s2=None, o2=None, R=(), W=(), B=()):
+        if o2 is None:
+            op("v", lambda: g.vector.tensor_scalar(o, i, s1, None, o1), R, W, B)
+        else:
+            op("v", lambda: g.vector.tensor_scalar(o, i, s1, s2, o1, o2), R, W, B)
+
+    def tt(o, a, b, o1, R=(), W=(), B=()):
+        op("v", lambda: g.vector.tensor_tensor(o, a, b, o1), R, W, B)
+
+    def cp(o, i, R=(), W=(), B=()):
+        op("v", lambda: g.vector.tensor_copy(o, i), R, W, B)
+
+    def scan(o, i, n, R=(), W=(), B=()):
+        op("v", lambda: g.vector.tensor_tensor_scan(o, i, v("zf", 0, n), 0.0, A.add, A.add), tuple(R) + ("zf",), W, B)
+
+    def fill(o, c, W):
+        op("v", lambda: g.vector.memset(o, c), (), W)
+
+    def act(o, i, f, R=(), W=(), B=(), **k):
+        op("s", lambda: g.scalar.activation(o, i, f, **k), R, W, B)
+
+    def quant(name, a, b, tile, R, W):
+        op("v", lambda: g.vector.quantize_mx(v(name, a, b), v(name + "s", a, b), tile), R, W)
+
+    def ps(bank, n):
+        return T.ps[:, 512 * bank:512 * bank + n]
+
+    def mm(bank, n, l, la, r, ra, R, start=True, stop=True):
+        op("p", lambda: g.tensor.matmul_mx(ps(bank, n), v(l, la, la + 128), v(l + "s", la, la + 128),
+                                           v(r, ra, ra + n), v(r + "s", ra, ra + n), start, stop), R, (), (bank,))
+
+    def iota(name, pattern, base=0, cm=0, n=None):
+        o = v(name, 0, n)
+        if name in ("ci", "ru"):
+            op("g", lambda: g.iota(o, pattern, base, cm), (), (name,))
+        else:
+            op("g", lambda: g.iota(o, pattern, base, cm, allow_small_or_imprecise_dtypes=True), (), (name,))
+
+    dma("y", "dx", [(T.xt[:, :], T.x[:, :])], (), ("xt",))
+    dma("y", "du", [(T.ut[:, :], T.u[:, :])], (), ("ut",))
+    dma("y", "dw", [(T.wq[:, :].bitcast(dt.uint8), T.wc[:, :]), (T.wqs[:, :], T.ws[:, :])], (), ("wq",))
+    dma("y", "dv", [(T.vt[:, :], T.v[:, :])], (), ("vt",))
+    iota("ci", [[1, 1]], 0, 1, 1)
+    iota("ru", [[16, 8]])
+    iota("r256", [[0, 2], [1, 128]])
+    iota("r18", [[1, 16], [0, 18]])
+    iota("zf", [[0, C]])
+    iota("rg4", [[1, 8], [0, 64]])
+    iota("rr", [[1, 8], [8, 4], [0, 4]])
+    iota("rv", [[0, 18], [1, 4], [0, 4]])
+    iota("rs", [[0, 18], [1, 4]])
+    iota("rt", [[16, 72]], 576)
+    iota("ry", [[0, 2], [64, 36]])
+    iota("r4c", [[4, 18]])
+    iota("scw", [[0, 2816]])
+    iota("rp", [[4, C]], 576)
+
+    fill(v("wk"), 0.0, ("wk",))
+    cp(v("ul"), v("ru"), ("ru",), ("ul",))
+    ts(v("ci", 1, 2), v("ci", 0, 1), 15, A.bitwise_and, R=("ci",), W=("ci1",))
+    ts(v("ci", 2, 3), v("ci", 0, 1), 4, A.arith_shift_right, R=("ci",), W=("ci2",))
+    ts(v("ci", 3, 4), v("ci", 0, 1), 2, A.arith_shift_right, 3, A.bitwise_and, R=("ci",), W=("ci3",))
+    ts(v("ci", 4, 5), v("ci", 0, 1), 3, A.bitwise_and, R=("ci",), W=("ci4",))
+    cp(v("cf", 0, 5), v("ci", 0, 5), ("ci", "ci1", "ci2", "ci3", "ci4"), ("cf",))
+    cP, cI, cG, cR, cA = [v("cf", k, k + 1) for k in range(5)]
+    ts(v("wk", 3, 1024, 4), v("r256"), cP, A.is_equal, R=("r256", "cf"), W=("wk",))
+    for b in range(4):
+        quant("idq%d" % b, 0, 256, v("wk", 3 - b, 1027 - b), ("wk",), ("idq%d" % b,))
+    quant("uq", 0, 128, T.ut[:, 0:512], ("ut",), ("uq",))
+    cp(T.urq[:, 0:128].bitcast(dt.uint32), T.uq[:, 0:128].bitcast(dt.uint32).indirect(T.ul[:, 0:8]), ("uq", "ul"), ("urq",))
+    cp(T.urqs[:, 0:128], T.uqs[:, 0:128].indirect(T.ul[:, 0:8]), ("uq", "ul"), ("urqs",))
+    ts(v("mo"), v("r18"), cI, A.is_equal, R=("r18", "cf"), W=("mo",))
+    for b in (2, 3):
+        act(T.fl4[:, b:4 * C:4], v("zf"), F.Copy, ("zf",), ("fl4%d" % b,))
+    act(T.fe[:, 288:512], v("zf", 0, 224), F.Copy, ("zf",), ("fez",))
+    for k in range(4):
+        act(v("clz", 240 * k, 240 * k + 240), v("zf", 0, 240), F.Copy, ("zf",), ("clz",))
+    edges = []
+    for e in list(range(4)) + list(range(1152, TB)):
+        fill(T.tw[:, e:e + 7 * TB + 1:TB], 0.0, ("twz%d" % e,))
+        edges.append("twz%d" % e)
+    t0 = ["tw0%d" % b for b in range(4)]
+
+    def group_constants():
+        ts(v("cgb"), v("rg4"), cG, A.is_equal, R=("rg4", "cf"), W=("cgb",))
+        quant("gbq", 0, 128, v("cgb"), ("cgb",), ("gbq",))
+        ts(v("cga"), v("cgb"), 2.0, A.mult, R=("cgb",), W=("cga",))
+        quant("gaq", 0, 128, v("cga"), ("cga",), ("gaq",))
+
+    def list_constants():
+        def col(k):
+            return v("cx", k, k + 1)
+        for b in range(4):
+            ts(col(5 + b), cG, float(8 * b), A.add, R=("cf",), W=("cx%d" % (5 + b),))
+        fill(v("cs1"), 0.0625, ("cs1",))
+        c2, c3 = ["cs2%d" % b for b in range(4)], ["cs3%d" % b for b in range(4)]
+        for b in range(4):
+            ts(v("cs2", b, 512, 4), v("rr"), col(5 + b), A.is_le, 0.0625, A.mult, R=("rr", "cx%d" % (5 + b)), W=(c2[b],))
+            ts(v("cs3", b, 512, 4), v("rr"), col(5 + b), A.is_equal, -0.125, A.mult, R=("rr", "cx%d" % (5 + b)), W=(c3[b],))
+        ts(v("cs4"), v("cs3"), -576.0, A.mult, R=c3, W=("cs4",))
+        quant("s1q", 0, 128, v("cs1"), ("cs1",), ("s1q",))
+        quant("s2q", 0, 128, v("cs2"), c2, ("s2q",))
+        quant("s3q", 0, 128, v("cs3"), c3, ("s3q",))
+        quant("s4q", 0, 128, v("cs4"), ("cs4",), ("s4q",))
+        ts(col(0), cG, -1.0, A.mult, 8.0, A.add, R=("cf",), W=("cx0",))
+        ts(col(1), cR, 4.0, A.mult, R=("cf",), W=("cx1",))
+        ts(col(3), cR, 16.0, A.mult, R=("cf",), W=("cx3",))
+        ts(col(9), cA, 0.5, A.is_ge, 15.0, A.mult, R=("cf",), W=("cx9",))
+        ts(col(10), cA, 1.5, A.is_ge, 15.0, A.mult, R=("cf",), W=("cx10",))
+        ts(col(11), cA, 2.5, A.is_ge, 15.0, A.mult, R=("cf",), W=("cx11",))
+        ts(col(2), cG, 0.5, A.mult, col(1), A.add, R=("cf", "cx1"), W=("cx2",))
+        ts(col(12), col(9), 1.0, A.add, 1.5 * 2.0 ** 22, A.mult, R=("cx9",), W=("cx12",))
+        ts(col(4), cG, 8.0, A.add, col(3), A.add, R=("cf", "cx3"), W=("cx4",))
+        ts(col(13), col(10), 1.0, A.add, col(12), A.mult, R=("cx10", "cx12"), W=("cx13",))
+        ts(v("mv"), v("rv"), cR, A.is_equal, R=("rv", "cf"), W=("mv",))
+        ts(col(14), col(11), 1.0, A.add, col(13), A.mult, R=("cx11", "cx13"), W=("cx14",))
+        ts(v("vl"), v("r4c"), cA, A.add, R=("r4c", "cf"), W=("vl",))
+        ts(col(15), col(14), 16.0, A.mult, R=("cx14",), W=("cx15",))
+        ts(col(16), cG, 0.5, A.mult, R=("cf",), W=("cx16",))
+        for b in range(4):
+            a = 4 * (112 + 4 * b) + b
+            fill(v("clz", a, a + 13, 4), 2.0, ("clz",))
+        quant("lzq", 0, 240, v("clz"), ("clz",), ("lzq",))
+        ts(v("ms"), v("rs"), cA, A.is_equal, R=("rs", "cf"), W=("ms",))
+        ts(v("nc"), v("rt"), col(2), A.add, R=("rt", "cx2"), W=("nc",))
+        ts(v("yc"), v("ry"), col(4), A.add, R=("ry", "cx4"), W=("yc",))
+
+    def send(dst, arrive, left, src, land):
+        both = topo.mask(core, dst) & topo.mask(core, T.cores[rank ^ MASK[0]])
+        ne = bin(both).count("1")
+        rid, pid = topo.addr(dst, core)
+        before("g", (src,), (), ())
+        g.remote_dma(T[land][:, 0:H].bitcast(dt.uint8), T[src][:, 0:H].bitcast(dt.uint8), T.sem[arrive], T.sem[left], pid, rid, both)
+        g.remote_dma(T[land + "s"][:, 0:H], T[src + "s"][:, 0:H], T.sem[arrive], T.sem[left], pid, rid, both)
+        total[left] = total[arrive] = 2 * ne
+        after("g", (src,), (), (), (left, 2 * ne))
+        last[land] = ([(arrive, 2 * ne)], [])
+
+    def layer(code, tile, split):
+        for b in range(4):
+            q = "s" if not split or b % 2 else "v"
+            bank = (4 + b) if q == "s" else b
+            mm(bank, H, "wq", 128 * b, code, 0, ("wq", code))
+            o = T[tile][:, b:4 * H:4]
+            if q == "s":
+                act(o, ps(bank, H), F.Relu, (), (tile + str(b),), (bank,), scale=0.03125)
+            else:
+                ts(o, ps(bank, H), 0.0, A.max, 0.03125, A.mult, W=(tile + str(b),), B=(bank,))
+
+    def unpack(code, base, tag):
+        for k in range(32):
+            s, b = k // 4, k % 4
+            q = "vs"[k % 2]
+            bank = (k // 2) % 4 + (4 if q == "s" else 0)
+            mm(bank, H, "idq%d" % b, 16 * s, code, 0, ("idq%d" % b, code))
+            o = T.vw[:, 1152 * s + base + b:1152 * s + base + 576:4]
+            if q == "s":
+                act(o, ps(bank, H), F.Copy, (), ("%s%d" % (tag, k),), (bank,))
+            else:
+                cp(o, ps(bank, H), (), ("%s%d" % (tag, k),), (bank,))
+
+    def sm(k):
+        return v("sm", k, k + 1)
+
+    for r in range(3):
+        dst = T.cores[rank ^ MASK[r]]
+        quant("q", 0, C, T.xt[:, 0:4 * C], ("xt",), ("q",))
+        for bank in (0, 4):
+            mm(bank, C, "urq", 0, "q", 0, ("urq", "urqs", "q"))
+        for b, bank in enumerate((2, 3, 5, 7)):
+            mm(bank, C, "idq%d" % b, 0, "q", 0, ("idq%d" % b, "q"))
+            act(T.tw[:, 4 + b:1156:4], ps(bank, C), F.Copy, edges, ("tw0%d" % b,), (bank,))
+        turns = []
+        for s in range(1, 8):
+            n = 128 - 16 * s
+            turns.append((T.tw[0:n, TB * s + 4:TB * s + 1156], T.tw[16 * s:128, 4:1156]))
+            turns.append((T.tw[n:128, TB * s:TB * s + 1152], T.tw[0:16 * s, 4:1156]))
+        dma("y", "tr%d" % r, turns, t0 + edges, ("twr",))
+        tt(v("mm"), ps(0, C), v("mo"), A.mult, ("mo",), ("mm",), (0,))
+        tt(v("f1"), v("mm", 0, 144), v("mm", 144, 288), A.add, ("mm",), ("f1",))
+        tt(v("f2"), v("f1", 0, 72), v("f1", 72, 144), A.add, ("f1",), ("f2",))
+        tt(v("f3"), v("f2", 0, 36), v("f2", 36, 72), A.add, ("f2",), ("f3",))
+        tt(v("own", 0, 18), v("f3", 0, 18), v("f3", 18, 36), A.add, ("f3",), ("own",))
+        for t in range(NV, 18):
+            k = t // 4
+            act(T["fl%d" % k][:, t % 4:4 * C:4], ps(4, C), F.Sign, ("own",), ("fl%d%d" % (k, t % 4),), (4,),
+                scale=-1.0, bias=T.own[:, t:t + 1])
+        if r == 0:
+            group_constants()
+        for k in range(5):
+            if k < 2:
+                for b in range(4):
+                    t = 4 * k + b
+                    ts(T["fl%d" % k][:, b:4 * C:4], ps(0, C), T.own[:, t:t + 1], A.is_lt, R=("own",), W=("fl%d%d" % (k, b),), B=(0,))
+            if r == 0 and k == 2:
+                list_constants()
+            quant("flq%d" % k, 0, C, T["fl%d" % k][:, 0:4 * C], ["fl%d%d" % (k, b) for b in range(4)], ("flq%d" % k,))
+            for bank in (6, 1):
+                w = "gaq" if k < 2 else "gbq"
+                mm(bank, C, w, 0, "flq%d" % k, 0, (w, "flq%d" % k), k == 0, k == 4)
+        act(v("junk"), ps(6, C), F.Sign, (), ("junk", "sm0"), (6,), scale=-1.0, bias=127.5, accum_out=sm(0))
+        ts(v("n1"), ps(1, C), 128.0, A.is_ge, -2048.0, A.mult, W=("n1",), B=(1,))
+        tt(v("m1"), ps(1, C), v("n1"), A.add, ("n1",), ("m1",), (1,))
+        op("v", lambda: g.vector.tensor_reduce(sm(1), v("m1"), X.X, A.max), ("m1",), ("sm1",))
+        op("v", lambda: g.vector.tensor_reduce(sm(2), v("m1"), X.X, A.min), ("m1",), ("sm2",))
+        ts(sm(3), sm(0), -0.5, A.is_ge, R=("sm0",), W=("sm3",))
+        tt(sm(4), sm(1), sm(2), A.subtract, ("sm1", "sm2"), ("sm4",))
+        ts(sm(6), sm(0), -1.0 / 2048, A.mult, 2048.0 + 1.0 / 2048, A.add, R=("sm0",), W=("sm6",))
+        ts(sm(5), sm(4), sm(3), A.mult, sm(2), A.add, R=("sm4", "sm3", "sm2"), W=("sm5",))
+        ts(sm(7), sm(3), -2048.0, A.mult, sm(6), A.add, R=("sm3", "sm6"), W=("sm7",))
+        ts(v("ec"), v("m1"), sm(5), A.is_equal, 1.0 / 1024, A.mult, R=("m1", "sm5"), W=("ec",))
+        tt(sm(8), sm(7), sm(5), A.add, ("sm7", "sm5"), ("sm8",))
+        scan(v("hs"), v("ec"), C, ("ec",), ("hs",))
+        ts(sm(9), v("hs", 287, 288), sm(3), A.mult, sm(8), A.add, R=("hs", "sm3", "sm8"), W=("sm9",))
+        tt(v("key"), ps(1, C), v("hs"), A.add, ("hs",), ("key",), (1,))
+        ts(T.fe[:, 0:C], v("key"), sm(9), A.is_lt, 0.5, A.subtract, R=("key", "sm9"), W=("fe",))
+        quant("nq", 0, 128, T.fe[:, 0:512], ("fe", "fez"), ("nq",))
+        for bank, w in ((2, "s1q"), (3, "s2q"), (5, "s3q"), (7, "s4q")):
+            mm(bank, 128, w, 0, "nq", 0, (w, "nq"))
+        scan(v("cc"), ps(2, 72), 72, (), ("cc",), (2,))
+        tt(v("xx"), v("cc"), ps(3, 72), A.subtract, ("cc",), ("xx",), (3,))
+        tt(v("zz"), v("xx"), ps(5, 72), A.mult, ("xx",), ("zz",), (5,))
+        ma, mb = v("cx", 14, 15), v("cx", 15, 16)
+        tt(v("t2"), v("zz"), ps(7, 72), A.add, ("zz",), ("t2",), (7,))
+        ts(v("ra"), v("zz"), ma, A.add, ma, A.subtract, R=("zz", "cx14"), W=("ra",))
+        tt(v("nn"), v("nc"), v("t2"), A.subtract, ("nc", "t2"), ("nn",))
+        ts(v("rb"), v("zz"), mb, A.add, mb, A.subtract, R=("zz", "cx15"), W=("rb",))
+        tt(v("sl0"), v("nn"), v("ms"), A.mult, ("nn", "ms"), ("sl0",))
+        tt(T.dg[:, 0:72], v("ra"), v("rb"), A.subtract, ("ra", "rb"), ("dg",))
+        tt(v("sl1"), v("sl0", 0, 72, 2), v("sl0", 1, 72, 2), A.add, ("sl0",), ("sl1",))
+        tt(v("n18"), v("sl1", 0, 36, 2), v("sl1", 1, 36, 2), A.add, ("sl1",), ("n18",))
+        tt(T.val[:, 0:C], T.dg[:, 0:72].indirect(T.vl[:, 0:18]), v("mv"), A.mult, ("dg", "vl", "mv"), ("val",))
+        ts(v("h18"), v("n18"), 7, A.bitwise_and, R=("n18",), W=("h18",))
+        ts(v("w1"), v("n18"), 0.125, A.mult, R=("n18",), W=("w1",))
+        ts(v("v1"), v("h18"), 287.875, A.mult, R=("h18",), W=("v1",))
+        tt(v("e1"), v("v1"), v("w1"), A.add, ("v1", "w1"), ("e1",))
+        cp(T.sl[:, 0:18], v("e1"), ("e1",), ("sl",))
+        if r == 0:
+            quant("scq", 576, 704, T.scw[:, 2304:2816], ("scw",), ("scqp",))
+        cp(T.scw[:, 0:2304].indirect(T.sl[:, 0:18]), T.val[:, 0:C], ("sl", "val"), ("scw",))
+        for k in range(2):
+            quant("scq", 288 * k, 288 * k + 288, T.scw[:, 1152 * k:1152 * k + 1152], ("scw",), ("scq%d" % k,))
+        for h in range(8):
+            a = 72 * h
+            R = ["lzq"] + (["scq0"] if a < 288 else []) + (["scq1"] if a + 128 > 288 else []) + (["scqp"] if a + 128 > 576 else [])
+            mm(0, 128, "lzq", 112 - 16 * h, "scq", a, R, h == 0, h == 7)
+        tt(v("yi"), v("yc"), ps(0, 72), A.add, ("yc",), ("yi",), (0,))
+        ts(v("si"), v("yi"), 7, A.bitwise_and, R=("yi",), W=("si",))
+        ts(v("o1"), v("yi"), 0.5, A.mult, cA, A.add, R=("yi", "cf"), W=("o1",))
+        ts(v("o2"), v("si"), TB - 0.5, A.mult, R=("si",), W=("o2",))
+        tt(v("o3"), v("o1"), v("o2"), A.add, ("o1", "o2"), ("o3",))
+        cp(T.off[:, 0:72], v("o3"), ("o3",), ("off",))
+        win = t0 + edges + ["twr"]
+        cp(T.gt[:, 0:576], T.tw[:, 0:8 * TB].indirect(T.off[:, 36:72]), win + ["off"], ("gt",))
+        quant("gq", 0, H, T.gt[:, 0:576], ("gt",), ("gq",))
+        send(dst, "ga%d" % r, "sg%d" % r, "gq", "lg%d" % r)
+        cp(T.ft[:, 0:576], T.tw[:, 0:8 * TB].indirect(T.off[:, 0:36]), win + ["off"], ("ft",))
+        quant("fq", 0, H, T.ft[:, 0:576], ("ft",), ("fq",))
+        layer("fq", "at", False)
+        ts(v("yn"), v("nn"), v("cx", 0, 1), A.add, R=("nn", "cx0"), W=("yn",))
+        cp(v("ni"), v("nn"), ("nn",), ("ni",))
+        ts(v("sn"), v("yn"), 7, A.bitwise_and, R=("yn",), W=("sn",))
+        ts(v("cn"), v("ni"), 3, A.arith_shift_right, R=("ni",), W=("cn",))
+        ts(v("p1"), v("sn"), 1152.0, A.mult, R=("sn",), W=("p1",))
+        ts(v("p2"), v("cn"), 4.0, A.mult, cA, A.add, R=("cn", "cf"), W=("p2",))
+        tt(v("p3"), v("p1"), v("p2"), A.add, ("p1", "p2"), ("p3",))
+        cp(T.off2[:, 0:72], v("p3"), ("p3",), ("off2",))
+        quant("aq", 0, H, T.at[:, 0:576], ["at%d" % b for b in range(4)], ("aq",))
+        if r == 0:
+            quant("vq", 0, 128, T.vt[:, 0:512], ("vt",), ("vq",))
+        layer("lg%d" % r, "bt", True)
+        quant("bq", 0, H, T.bt[:, 0:576], ["bt%d" % b for b in range(4)], ("bq",))
+        send(dst, "bl%d" % r, "sb%d" % r, "bq", "lb%d" % r)
+        if r < 2:
+            op("g", lambda: g.iota(T.scw[:, 0:2304], [[0, 2304]], 0, 0, allow_small_or_imprecise_dtypes=True), (), ("scw",))
+        unpack("aq", 0, "va")
+        if r == 2:
+            for b in range(1, 4):
+                act(T.fe2[:, b:4 * C:4], v("zf"), F.Copy, ("zf",), ("fe2%d" % b,))
+            act(T.fe2[:, 0:4 * C:4], T.fe[:, 0:C], F.Copy, ("fe",), ("fe20",))
+            quant("f2q", 0, C, T.fe2[:, 0:4 * C], ["fe2%d" % b for b in range(4)], ("f2q",))
+            mm(0, C, "s1q", 0, "f2q", 0, ("s1q", "f2q"))
+            mm(1, C, "s2q", 0, "f2q", 0, ("s2q", "f2q"))
+            scan(v("cr"), ps(0, C), C, (), ("cr",), (0,))
+            tt(v("xr"), v("cr"), ps(1, C), A.subtract, ("cr",), ("xr",), (1,))
+            ts(v("pc"), v("rp"), v("cx", 16, 17), A.add, R=("rp", "cx16"), W=("pc",))
+            ts(v("yr"), v("xr"), 2.0, A.mult, -1152.0, A.add, R=("xr",), W=("yr",))
+            tt(v("zr"), v("yr"), T.fe[:, 0:C], A.mult, ("yr", "fe"), ("zr",))
+            tt(v("nr"), v("zr"), v("pc"), A.add, ("zr", "pc"), ("nr",))
+            buf, at, w = _SHARE["nr"]
+            dma("y", "oo", [(T.op[k:k + 1, 0:C], T[buf][16 * k:16 * k + 1, at:at + C]) for k in range(8)], ("nr",), ())
+        unpack("lb%d" % r, 576, "vb")
+        tt(T.xt[:, 0:4 * C], T.vw[:, 0:8 * 4 * C].indirect(T.off2[:, 0:72]), T.tw[:, 4:1156], A.add,
+           ["va%d" % k for k in range(32)] + ["vb%d" % k for k in range(32)] + ["off2"] + t0, ("xt",))
+
+    quant("q", 0, C, T.xt[:, 0:4 * C], ("xt",), ("q",))
+    mm(0, C, "vq", 0, "q", 0, ("vq", "q"))
+    cp(T.yo[:, 0:C], ps(0, C), (), ("yo",), (0,))
+    dma("y", "oq", [(T.oc[:, 0:4 * C], T.q[:, 0:C].bitcast(dt.uint8))]
+        + [(T.osc[4 * k:4 * k + 4, 0:C], T.qs[32 * k:32 * k + 4, 0:C]) for k in range(4)], ("q",), ())
+    dma("s", "oy", [(T.y[:, 0:C], T.yo[:, 0:C])], ("yo",), ())
+    for s, n in total.items():
+        if seen.get(("g", s), 0) < n:
+            g.wait_ge(T.sem[s], n)

@@ -3,7 +3,9 @@ from concourse.mybir import dt, AluOpType, AxisListType, ActivationFunctionType
 MASK = [4, 1, 2]
 C, H = 288, 144
 NV = 8
-TB = 1160
+TB = 4 * C
+BYDMA = [7, 6, 6]
+BDMA = 6
 F8, U8, BF, F32, I32, U16 = "float8_e4m3fn_x4", "uint8", "bfloat16", "float32", "int32", "uint16"
 
 SCRATCH = {}
@@ -35,22 +37,22 @@ _mx(*[("flq%d" % k, C) for k in range(5)], *[("idq%d" % k, 256) for k in range(4
 _mx(*[("%s%d" % (n, k), H) for n in ("lg", "lb") for k in range(3)])
 _add(BF, *[("fl%d" % k, 4 * C) for k in range(5)])
 _add(BF, ("xt", 4 * C), ("ut", 512), ("vt", 512), ("gt", 4 * H), ("ft", 4 * H), ("at", 4 * H), ("bt", 4 * H), ("tw", 8 * TB),
-     ("vw", 8 * 4 * C), ("scw", 2816), ("fe", 512), ("fe2", 4 * C), ("wk", 1032), ("val", C), ("junk", C))
+     ("vw", 8 * TB), ("scw", 2816), ("fe", 512), ("fe2", 4 * C), ("wk", 1032), ("val", C), ("junk", C))
 _pack("ctile", BF, ("cga", 512), ("cgb", 512), ("cs1", 512), ("cs2", 512), ("cs3", 512), ("cs4", 512), ("clz", 960))
-_pack("rows", F32, ("zf", C), ("r256", 256), ("r18", C), ("rg4", 512), ("rr", 128), ("rv", C), ("rs", 72), ("rt", 72), ("ry", 72),
-      ("r4c", 18), ("rp", C))
-_pack("cons", F32, ("cf", 8), ("cx", 32), ("mo", C), ("mv", C), ("ms", 72), ("nc", 72), ("yc", 72), ("pc", C))
-_pack("temp", F32, ("mm", C), ("f1", 144), ("f2", 72), ("f3", 36), ("n1", C), ("m1", C), ("ec", C), ("hs", C), ("key", C),
+_pack("rows", F32, ("zf", C), ("r256", 256), ("r16", C), ("rg4", 512), ("rr", 128), ("rv", C), ("rs", 72), ("rt", 72), ("ry", 72),
+      ("r4c", 18), ("rp", C), ("m0", C))
+_pack("cons", F32, ("cf", 8), ("cx", 40), ("mo", C), ("mv", C), ("ms", 72), ("nc", 72), ("yc", 72), ("pc", C))
+_pack("temp", F32, ("mm", C), ("n1", C), ("m1", C), ("ec", C), ("hs", C), ("key", C),
       ("sm", 32), ("cc", 72), ("xx", 72), ("zz", 72), ("t2", 72), ("nn", 72), ("ra", 72), ("rb", 72), ("sl0", 72), ("sl1", 36),
-      ("v1", 18), ("w1", 18), ("e1", 18), ("o1", 72), ("o2", 72), ("o3", 72), ("p1", 72), ("p2", 72), ("p3", 72), ("nr", C),
+      ("v1", 18), ("w1", 18), ("e1", 18), ("o1", 72), ("o2", 72), ("o3", 72), ("nr", C),
       ("cr", C), ("xr", C), ("yr", C), ("zr", C))
-_pack("ints", I32, ("ci", 8), ("ru", 8), ("n18", 18), ("h18", 18), ("yi", 72), ("si", 72), ("yn", 72), ("sn", 72), ("ni", 72), ("cn", 72))
-_add(F32, ("own", 24), ("dg", 72), ("yo", C))
+_pack("ints", I32, ("ci", 8), ("ru", 8), ("n18", 18), ("h18", 18), ("yi", 72), ("si", 72), ("ji", 72), ("ni", 72))
+_add(F32, ("ow", C), ("dg", 72), ("yo", C))
 _add(U16, ("ul", 8), ("vl", 18), ("sl", 18), ("off", 72), ("off2", 72))
 SCRATCH["ps"] = ("psum", [128, 4096], F32)
 
 SEMAPHORES = (["qv", "qs", "qp", "qg", "dx", "du", "dv", "dw", "oy", "oo", "oq"]
-              + ["%s%d" % (n, r) for n in ("tr", "ga", "bl", "sg", "sb") for r in range(3)])
+              + ["%s%d" % (n, r) for n in ("tr", "ta", "tb", "ga", "bl", "sg", "sb") for r in range(3)])
 
 
 def rank_program(g, core, T, topo):
@@ -115,9 +117,6 @@ def rank_program(g, core, T, topo):
     def scan(o, i, n, R=(), W=(), B=()):
         op("v", lambda: g.vector.tensor_tensor_scan(o, i, v("zf", 0, n), 0.0, A.add, A.add), tuple(R) + ("zf",), W, B)
 
-    def fill(o, c, W):
-        op("v", lambda: g.vector.memset(o, c), (), W)
-
     def act(o, i, f, R=(), W=(), B=(), **k):
         op("s", lambda: g.scalar.activation(o, i, f, **k), R, W, B)
 
@@ -131,101 +130,101 @@ def rank_program(g, core, T, topo):
         op("p", lambda: g.tensor.matmul_mx(ps(bank, n), v(l, la, la + 128), v(l + "s", la, la + 128),
                                            v(r, ra, ra + n), v(r + "s", ra, ra + n), start, stop), R, (), (bank,))
 
-    def iota(name, pattern, base=0, cm=0, n=None):
-        o = v(name, 0, n)
-        if name in ("ci", "ru"):
-            op("g", lambda: g.iota(o, pattern, base, cm), (), (name,))
+    def iota(o, pattern, key, base=0, cm=0, whole=False):
+        if whole:
+            op("g", lambda: g.iota(o, pattern, base, cm), (), (key,))
         else:
-            op("g", lambda: g.iota(o, pattern, base, cm, allow_small_or_imprecise_dtypes=True), (), (name,))
+            op("g", lambda: g.iota(o, pattern, base, cm, allow_small_or_imprecise_dtypes=True), (), (key,))
 
-    dma("y", "dx", [(T.xt[:, :], T.x[:, :])], (), ("xt",))
+    def row(name, pattern, base=0):
+        iota(v(name), pattern, name, base)
+
+    def turned(win, at, n, rots):
+        out = []
+        for s in rots:
+            k, a = 128 - 16 * s, TB * s + at
+            out.append((win[0:k, a:a + n], win[16 * s:128, at:at + n]))
+            out.append((win[k:128, a:a + n], win[0:16 * s, at:at + n]))
+        return out
+
     dma("y", "du", [(T.ut[:, :], T.u[:, :])], (), ("ut",))
-    dma("y", "dw", [(T.wq[:, :].bitcast(dt.uint8), T.wc[:, :]), (T.wqs[:, :], T.ws[:, :])], (), ("wq",))
-    dma("y", "dv", [(T.vt[:, :], T.v[:, :])], (), ("vt",))
-    iota("ci", [[1, 1]], 0, 1, 1)
-    iota("ru", [[16, 8]])
-    iota("r256", [[0, 2], [1, 128]])
-    iota("r18", [[1, 16], [0, 18]])
-    iota("zf", [[0, C]])
-    iota("rg4", [[1, 8], [0, 64]])
-    iota("rr", [[1, 8], [8, 4], [0, 4]])
-    iota("rv", [[0, 18], [1, 4], [0, 4]])
-    iota("rs", [[0, 18], [1, 4]])
-    iota("rt", [[16, 72]], 576)
-    iota("ry", [[0, 2], [64, 36]])
-    iota("r4c", [[4, 18]])
-    iota("scw", [[0, 2816]])
-    iota("rp", [[4, C]], 576)
+    dma("y", "dx", [(T.xt[:, :], T.x[:, :])], (), ("xt",))
+    iota(v("ci", 0, 1), [[1, 1]], "ci", 0, 1, True)
+    iota(v("ru"), [[16, 8]], "ru", 0, 0, True)
+    row("r256", [[0, 2], [1, 128]])
+    row("rr", [[1, 8], [8, 4], [0, 4]])
+    row("r16", [[0, 18], [1, 16]])
+    row("rg4", [[1, 8], [0, 64]])
+    row("zf", [[0, C]])
+    iota(T.fe[:, 288:512], [[0, 224]], "fez")
+    row("rt", [[16, 72]], 576)
+    row("ry", [[0, 2], [64, 36]])
+    row("r4c", [[4, 18]])
+    row("rv", [[0, 18], [1, 4], [0, 4]])
+    row("rs", [[0, 18], [1, 4]])
+    row("clz", [[0, 960]])
+    row("scw", [[0, 2816]])
+    row("rp", [[4, C]], 576)
 
-    fill(v("wk"), 0.0, ("wk",))
-    cp(v("ul"), v("ru"), ("ru",), ("ul",))
-    ts(v("ci", 1, 2), v("ci", 0, 1), 15, A.bitwise_and, R=("ci",), W=("ci1",))
+    op("v", lambda: g.vector.memset(v("wk"), 0.0), (), ("wk",))
     ts(v("ci", 2, 3), v("ci", 0, 1), 4, A.arith_shift_right, R=("ci",), W=("ci2",))
+    ts(v("ci", 1, 2), v("ci", 0, 1), 15, A.bitwise_and, R=("ci",), W=("ci1",))
     ts(v("ci", 3, 4), v("ci", 0, 1), 2, A.arith_shift_right, 3, A.bitwise_and, R=("ci",), W=("ci3",))
     ts(v("ci", 4, 5), v("ci", 0, 1), 3, A.bitwise_and, R=("ci",), W=("ci4",))
     cp(v("cf", 0, 5), v("ci", 0, 5), ("ci", "ci1", "ci2", "ci3", "ci4"), ("cf",))
     cP, cI, cG, cR, cA = [v("cf", k, k + 1) for k in range(5)]
+    cp(v("ul"), v("ru"), ("ru",), ("ul",))
     ts(v("wk", 3, 1024, 4), v("r256"), cP, A.is_equal, R=("r256", "cf"), W=("wk",))
     for b in range(4):
         quant("idq%d" % b, 0, 256, v("wk", 3 - b, 1027 - b), ("wk",), ("idq%d" % b,))
     quant("uq", 0, 128, T.ut[:, 0:512], ("ut",), ("uq",))
     cp(T.urq[:, 0:128].bitcast(dt.uint32), T.uq[:, 0:128].bitcast(dt.uint32).indirect(T.ul[:, 0:8]), ("uq", "ul"), ("urq",))
     cp(T.urqs[:, 0:128], T.uqs[:, 0:128].indirect(T.ul[:, 0:8]), ("uq", "ul"), ("urqs",))
-    ts(v("mo"), v("r18"), cI, A.is_equal, R=("r18", "cf"), W=("mo",))
+    ts(v("mo"), v("r16"), cI, A.is_equal, R=("r16", "cf"), W=("mo",))
+
+    def col(k):
+        return v("cx", k, k + 1)
+
+    def ccol(k, i, f, R, **kw):
+        act(col(k), i, f, R, ("cx%d" % k,), **kw)
+
+    c2, c3 = ["cs2%d" % b for b in range(4)], ["cs3%d" % b for b in range(4)]
+    for b in range(4):
+        ccol(5 + b, cG, F.Identity, ("cf",), bias=8.0 * b + 0.5)
+        ccol(22 + b, cG, F.Identity, ("cf",), bias=8.0 * b)
+    for b in range(4):
+        act(v("cs2", b, 512, 4), v("rr"), F.Sign, ("rr", "cx%d" % (5 + b)), (c2[b],), scale=-1.0, bias=col(5 + b))
+        act(v("cs3", b, 512, 4), v("rr"), F.Abs, ("rr", "cx%d" % (22 + b)), (c3[b],), scale=-1.0, bias=col(22 + b))
+    act(v("cs2"), v("cs2"), F.Identity, c2, ("cs2",), scale=0.03125, bias=0.03125)
+    act(v("cs3"), v("cs3"), F.Relu, c3, ("cs3",), scale=-1.0, bias=1.0)
+    act(v("m0"), v("r16"), F.Sign, ("r16",), ("m0",))
     for b in (2, 3):
         act(T.fl4[:, b:4 * C:4], v("zf"), F.Copy, ("zf",), ("fl4%d" % b,))
-    act(T.fe[:, 288:512], v("zf", 0, 224), F.Copy, ("zf",), ("fez",))
-    for k in range(4):
-        act(v("clz", 240 * k, 240 * k + 240), v("zf", 0, 240), F.Copy, ("zf",), ("clz",))
-    edges = []
-    for e in list(range(4)) + list(range(1152, TB)):
-        fill(T.tw[:, e:e + 7 * TB + 1:TB], 0.0, ("twz%d" % e,))
-        edges.append("twz%d" % e)
-    t0 = ["tw0%d" % b for b in range(4)]
+    t0, va = ["tw0%d" % b for b in range(4)], ["va%d" % k for k in range(4)]
 
-    def group_constants():
-        ts(v("cgb"), v("rg4"), cG, A.is_equal, R=("rg4", "cf"), W=("cgb",))
-        quant("gbq", 0, 128, v("cgb"), ("cgb",), ("gbq",))
-        ts(v("cga"), v("cgb"), 2.0, A.mult, R=("cgb",), W=("cga",))
-        quant("gaq", 0, 128, v("cga"), ("cga",), ("gaq",))
-
-    def list_constants():
-        def col(k):
-            return v("cx", k, k + 1)
-        for b in range(4):
-            ts(col(5 + b), cG, float(8 * b), A.add, R=("cf",), W=("cx%d" % (5 + b),))
-        fill(v("cs1"), 0.0625, ("cs1",))
-        c2, c3 = ["cs2%d" % b for b in range(4)], ["cs3%d" % b for b in range(4)]
-        for b in range(4):
-            ts(v("cs2", b, 512, 4), v("rr"), col(5 + b), A.is_le, 0.0625, A.mult, R=("rr", "cx%d" % (5 + b)), W=(c2[b],))
-            ts(v("cs3", b, 512, 4), v("rr"), col(5 + b), A.is_equal, -0.125, A.mult, R=("rr", "cx%d" % (5 + b)), W=(c3[b],))
-        ts(v("cs4"), v("cs3"), -576.0, A.mult, R=c3, W=("cs4",))
-        quant("s1q", 0, 128, v("cs1"), ("cs1",), ("s1q",))
-        quant("s2q", 0, 128, v("cs2"), c2, ("s2q",))
-        quant("s3q", 0, 128, v("cs3"), c3, ("s3q",))
-        quant("s4q", 0, 128, v("cs4"), ("cs4",), ("s4q",))
-        ts(col(0), cG, -1.0, A.mult, 8.0, A.add, R=("cf",), W=("cx0",))
-        ts(col(1), cR, 4.0, A.mult, R=("cf",), W=("cx1",))
-        ts(col(3), cR, 16.0, A.mult, R=("cf",), W=("cx3",))
-        ts(col(9), cA, 0.5, A.is_ge, 15.0, A.mult, R=("cf",), W=("cx9",))
-        ts(col(10), cA, 1.5, A.is_ge, 15.0, A.mult, R=("cf",), W=("cx10",))
-        ts(col(11), cA, 2.5, A.is_ge, 15.0, A.mult, R=("cf",), W=("cx11",))
-        ts(col(2), cG, 0.5, A.mult, col(1), A.add, R=("cf", "cx1"), W=("cx2",))
-        ts(col(12), col(9), 1.0, A.add, 1.5 * 2.0 ** 22, A.mult, R=("cx9",), W=("cx12",))
-        ts(col(4), cG, 8.0, A.add, col(3), A.add, R=("cf", "cx3"), W=("cx4",))
-        ts(col(13), col(10), 1.0, A.add, col(12), A.mult, R=("cx10", "cx12"), W=("cx13",))
-        ts(v("mv"), v("rv"), cR, A.is_equal, R=("rv", "cf"), W=("mv",))
-        ts(col(14), col(11), 1.0, A.add, col(13), A.mult, R=("cx11", "cx13"), W=("cx14",))
-        ts(v("vl"), v("r4c"), cA, A.add, R=("r4c", "cf"), W=("vl",))
-        ts(col(15), col(14), 16.0, A.mult, R=("cx14",), W=("cx15",))
-        ts(col(16), cG, 0.5, A.mult, R=("cf",), W=("cx16",))
-        for b in range(4):
-            a = 4 * (112 + 4 * b) + b
-            fill(v("clz", a, a + 13, 4), 2.0, ("clz",))
-        quant("lzq", 0, 240, v("clz"), ("clz",), ("lzq",))
-        ts(v("ms"), v("rs"), cA, A.is_equal, R=("rs", "cf"), W=("ms",))
-        ts(v("nc"), v("rt"), col(2), A.add, R=("rt", "cx2"), W=("nc",))
-        ts(v("yc"), v("ry"), col(4), A.add, R=("ry", "cx4"), W=("yc",))
+    def more_constants():
+        act(v("cs4"), v("cs3"), F.Copy, ("cs3",), ("cs4",), scale=72.0)
+        act(v("cs3"), v("cs3"), F.Copy, ("cs3",), ("cs3",), scale=-0.125)
+        ccol(1, cR, F.Copy, ("cf",), scale=4.0)
+        ccol(3, cR, F.Copy, ("cf",), scale=16.0)
+        for k in range(3):
+            ccol(26 + k, cA, F.Identity, ("cf",), bias=-0.5 - k)
+        ccol(2, cG, F.Identity, ("cf", "cx1"), scale=0.5, bias=col(1))
+        ccol(4, cG, F.Identity, ("cf", "cx3"), scale=2.0, bias=col(3))
+        for k in range(3):
+            ccol(9 + k, col(26 + k), F.Sign, ("cx%d" % (26 + k),))
+        act(v("nc"), v("rt"), F.Identity, ("rt", "cx2"), ("nc",), bias=col(2))
+        act(v("yc"), v("ry"), F.Identity, ("ry", "cx4"), ("yc",), bias=col(4))
+        for k in range(3):
+            ccol(17 + k, col(9 + k), F.Identity, ("cx%d" % (9 + k),), scale=7.5, bias=8.5)
+        ccol(12, col(17), F.Copy, ("cx17",), scale=1.5 * 2.0 ** 22)
+        ccol(13, col(18), F.Copy, ("cx18", "cx12"), scale=col(12))
+        ccol(14, col(19), F.Copy, ("cx19", "cx13"), scale=col(13))
+        ccol(15, col(14), F.Copy, ("cx14",), scale=16.0)
+        ccol(20, col(14), F.Copy, ("cx14",), scale=-1.0)
+        ccol(21, col(14), F.Copy, ("cx14",), scale=-16.0)
+        ccol(0, cG, F.Identity, ("cf",), scale=-1.0, bias=8.0)
+        ccol(16, cG, F.Copy, ("cf",), scale=0.5)
 
     def send(dst, arrive, left, src, land):
         both = topo.mask(core, dst) & topo.mask(core, T.cores[rank ^ MASK[0]])
@@ -249,17 +248,32 @@ def rank_program(g, core, T, topo):
             else:
                 ts(o, ps(bank, H), 0.0, A.max, 0.03125, A.mult, W=(tile + str(b),), B=(bank,))
 
-    def unpack(code, base, tag):
-        for k in range(32):
+    def unpack(code, base, tag, lo, hi):
+        for k in range(lo, hi):
             s, b = k // 4, k % 4
             q = "vs"[k % 2]
             bank = (k // 2) % 4 + (4 if q == "s" else 0)
             mm(bank, H, "idq%d" % b, 16 * s, code, 0, ("idq%d" % b, code))
-            o = T.vw[:, 1152 * s + base + b:1152 * s + base + 576:4]
+            o = T.vw[:, TB * s + base + b:TB * s + base + 576:4]
             if q == "s":
                 act(o, ps(bank, H), F.Copy, (), ("%s%d" % (tag, k),), (bank,))
             else:
                 cp(o, ps(bank, H), (), ("%s%d" % (tag, k),), (bank,))
+
+    def turn(r, lo, hi):
+        for k in range(lo, min(hi, 4 * (7 - BYDMA[r]))):
+            s, b = 1 + BYDMA[r] + k // 4, k % 4
+            mm(4 + k % 3, C, "idq%d" % b, 16 * s, "q", 0, ("idq%d" % b, "q"))
+            act(T.tw[:, TB * s + b:TB * s + TB:4], ps(4 + k % 3, C), F.Copy, (), ("tw%d%d" % (s, b),), (4 + k % 3,))
+
+    def offsets(out):
+        ts(v("yi"), v("ni"), col(0), A.add, R=("ni", "cx0"), W=("yi",))
+        ts(v("ji"), v("ni"), 3, A.arith_shift_right, R=("ni",), W=("ji",))
+        ts(v("si"), v("yi"), 7, A.bitwise_and, R=("yi",), W=("si",))
+        ts(v("o1"), v("ji"), 4.0, A.mult, cA, A.add, R=("ji", "cf"), W=("o1",))
+        ts(v("o2"), v("si"), float(TB), A.mult, R=("si",), W=("o2",))
+        tt(v("o3"), v("o1"), v("o2"), A.add, ("o1", "o2"), ("o3",))
+        cp(T[out][:, 0:72], v("o3"), ("o3",), (out,))
 
     def sm(k):
         return v("sm", k, k + 1)
@@ -271,45 +285,45 @@ def rank_program(g, core, T, topo):
             mm(bank, C, "urq", 0, "q", 0, ("urq", "urqs", "q"))
         for b, bank in enumerate((2, 3, 5, 7)):
             mm(bank, C, "idq%d" % b, 0, "q", 0, ("idq%d" % b, "q"))
-            act(T.tw[:, 4 + b:1156:4], ps(bank, C), F.Copy, edges, ("tw0%d" % b,), (bank,))
-        turns = []
-        for s in range(1, 8):
-            n = 128 - 16 * s
-            turns.append((T.tw[0:n, TB * s + 4:TB * s + 1156], T.tw[16 * s:128, 4:1156]))
-            turns.append((T.tw[n:128, TB * s:TB * s + 1152], T.tw[0:16 * s, 4:1156]))
-        dma("y", "tr%d" % r, turns, t0 + edges, ("twr",))
+            act(T.tw[:, b:TB:4], ps(bank, C), F.Copy, (), ("tw0%d" % b,), (bank,))
+        dma("y", "tr%d" % r, turned(T.tw, 0, TB, range(1, 1 + BYDMA[r])), t0, ("twr",))
+        if r == 0:
+            dma("y", "dw", [(T.wq[:, :].bitcast(dt.uint8), T.wc[:, :]), (T.wqs[:, :], T.ws[:, :])], (), ("wq",))
+            dma("y", "dv", [(T.vt[:, :], T.v[:, :])], (), ("vt",))
+            ts(v("cgb"), v("rg4"), cG, A.is_equal, R=("rg4", "cf"), W=("cgb",))
+            ts(v("cga"), v("cgb"), 2.0, A.mult, R=("cgb",), W=("cga",))
         tt(v("mm"), ps(0, C), v("mo"), A.mult, ("mo",), ("mm",), (0,))
-        tt(v("f1"), v("mm", 0, 144), v("mm", 144, 288), A.add, ("mm",), ("f1",))
-        tt(v("f2"), v("f1", 0, 72), v("f1", 72, 144), A.add, ("f1",), ("f2",))
-        tt(v("f3"), v("f2", 0, 36), v("f2", 36, 72), A.add, ("f2",), ("f3",))
-        tt(v("own", 0, 18), v("f3", 0, 18), v("f3", 18, 36), A.add, ("f3",), ("own",))
+        op("v", lambda: g.vector.tensor_tensor_scan(v("ow"), v("m0"), v("mm"), 0.0, A.mult, A.add), ("m0", "mm"), ("ow",))
         for t in range(NV, 18):
             k = t // 4
-            act(T["fl%d" % k][:, t % 4:4 * C:4], ps(4, C), F.Sign, ("own",), ("fl%d%d" % (k, t % 4),), (4,),
-                scale=-1.0, bias=T.own[:, t:t + 1])
-        if r == 0:
-            group_constants()
+            act(T["fl%d" % k][:, t % 4:4 * C:4], ps(4, C), F.Sign, ("ow",), ("fl%d%d" % (k, t % 4),), (4,),
+                scale=-1.0, bias=v("ow", 16 * t + 15, 16 * t + 16))
         for k in range(5):
             if k < 2:
                 for b in range(4):
-                    t = 4 * k + b
-                    ts(T["fl%d" % k][:, b:4 * C:4], ps(0, C), T.own[:, t:t + 1], A.is_lt, R=("own",), W=("fl%d%d" % (k, b),), B=(0,))
-            if r == 0 and k == 2:
-                list_constants()
+                    a = 16 * (4 * k + b) + 15
+                    ts(T["fl%d" % k][:, b:4 * C:4], ps(0, C), v("ow", a, a + 1), A.is_lt, R=("ow",), W=("fl%d%d" % (k, b),), B=(0,))
+            if r == 0 and k == 0:
+                quant("gaq", 0, 128, v("cga"), ("cga",), ("gaq",))
+                quant("gbq", 0, 128, v("cgb"), ("cgb",), ("gbq",))
             quant("flq%d" % k, 0, C, T["fl%d" % k][:, 0:4 * C], ["fl%d%d" % (k, b) for b in range(4)], ("flq%d" % k,))
-            for bank in (6, 1):
+            for bank in (1, 6):
                 w = "gaq" if k < 2 else "gbq"
                 mm(bank, C, w, 0, "flq%d" % k, 0, (w, "flq%d" % k), k == 0, k == 4)
         act(v("junk"), ps(6, C), F.Sign, (), ("junk", "sm0"), (6,), scale=-1.0, bias=127.5, accum_out=sm(0))
+        act(sm(10), sm(0), F.Sign, ("sm0",), ("sm10",), bias=0.5)
+        act(sm(6), sm(0), F.Identity, ("sm0",), ("sm6",), scale=-1.0 / 2048, bias=2048.0 + 1.0 / 2048)
+        act(sm(3), sm(10), F.Relu, ("sm10",), ("sm3",))
+        act(sm(7), sm(3), F.Identity, ("sm3", "sm6"), ("sm7",), scale=-2048.0, bias=sm(6))
+        if r == 0:
+            more_constants()
+        turn(r, 0, 28)
         ts(v("n1"), ps(1, C), 128.0, A.is_ge, -2048.0, A.mult, W=("n1",), B=(1,))
         tt(v("m1"), ps(1, C), v("n1"), A.add, ("n1",), ("m1",), (1,))
         op("v", lambda: g.vector.tensor_reduce(sm(1), v("m1"), X.X, A.max), ("m1",), ("sm1",))
         op("v", lambda: g.vector.tensor_reduce(sm(2), v("m1"), X.X, A.min), ("m1",), ("sm2",))
-        ts(sm(3), sm(0), -0.5, A.is_ge, R=("sm0",), W=("sm3",))
         tt(sm(4), sm(1), sm(2), A.subtract, ("sm1", "sm2"), ("sm4",))
-        ts(sm(6), sm(0), -1.0 / 2048, A.mult, 2048.0 + 1.0 / 2048, A.add, R=("sm0",), W=("sm6",))
         ts(sm(5), sm(4), sm(3), A.mult, sm(2), A.add, R=("sm4", "sm3", "sm2"), W=("sm5",))
-        ts(sm(7), sm(3), -2048.0, A.mult, sm(6), A.add, R=("sm3", "sm6"), W=("sm7",))
         ts(v("ec"), v("m1"), sm(5), A.is_equal, 1.0 / 1024, A.mult, R=("m1", "sm5"), W=("ec",))
         tt(sm(8), sm(7), sm(5), A.add, ("sm7", "sm5"), ("sm8",))
         scan(v("hs"), v("ec"), C, ("ec",), ("hs",))
@@ -317,83 +331,92 @@ def rank_program(g, core, T, topo):
         tt(v("key"), ps(1, C), v("hs"), A.add, ("hs",), ("key",), (1,))
         ts(T.fe[:, 0:C], v("key"), sm(9), A.is_lt, 0.5, A.subtract, R=("key", "sm9"), W=("fe",))
         quant("nq", 0, 128, T.fe[:, 0:512], ("fe", "fez"), ("nq",))
-        for bank, w in ((2, "s1q"), (3, "s2q"), (5, "s3q"), (7, "s4q")):
+        if r == 0:
+            op("v", lambda: g.vector.memset(v("cs1"), 0.0625), (), ("cs1",))
+            for k in range(1, 5):
+                quant("s%dq" % k, 0, 128, v("cs%d" % k), ("cs%d" % k,), ("s%dq" % k,))
+        for bank, w in ((2, "s1q"), (3, "s2q"), (0, "s3q"), (7, "s4q")):
             mm(bank, 128, w, 0, "nq", 0, (w, "nq"))
         scan(v("cc"), ps(2, 72), 72, (), ("cc",), (2,))
         tt(v("xx"), v("cc"), ps(3, 72), A.subtract, ("cc",), ("xx",), (3,))
-        tt(v("zz"), v("xx"), ps(5, 72), A.mult, ("xx",), ("zz",), (5,))
-        ma, mb = v("cx", 14, 15), v("cx", 15, 16)
+        tt(v("zz"), v("xx"), ps(0, 72), A.mult, ("xx",), ("zz",), (0,))
+        act(v("rb"), v("zz"), F.Identity, ("zz", "cx15"), ("rb",), bias=col(15))
+        act(v("ra"), v("zz"), F.Identity, ("zz", "cx14"), ("ra",), bias=col(14))
+        act(v("rb"), v("rb"), F.Identity, ("rb", "cx21"), ("rb",), bias=col(21))
+        act(v("ra"), v("ra"), F.Identity, ("ra", "cx20"), ("ra",), bias=col(20))
+        if r == 0:
+            ts(v("ms"), v("rs"), cA, A.is_equal, R=("rs", "cf"), W=("ms",))
         tt(v("t2"), v("zz"), ps(7, 72), A.add, ("zz",), ("t2",), (7,))
-        ts(v("ra"), v("zz"), ma, A.add, ma, A.subtract, R=("zz", "cx14"), W=("ra",))
         tt(v("nn"), v("nc"), v("t2"), A.subtract, ("nc", "t2"), ("nn",))
-        ts(v("rb"), v("zz"), mb, A.add, mb, A.subtract, R=("zz", "cx15"), W=("rb",))
         tt(v("sl0"), v("nn"), v("ms"), A.mult, ("nn", "ms"), ("sl0",))
-        tt(T.dg[:, 0:72], v("ra"), v("rb"), A.subtract, ("ra", "rb"), ("dg",))
         tt(v("sl1"), v("sl0", 0, 72, 2), v("sl0", 1, 72, 2), A.add, ("sl0",), ("sl1",))
+        if r == 0:
+            ts(v("mv"), v("rv"), cR, A.is_equal, R=("rv", "cf"), W=("mv",))
+            ts(v("vl"), v("r4c"), cA, A.add, R=("r4c", "cf"), W=("vl",))
         tt(v("n18"), v("sl1", 0, 36, 2), v("sl1", 1, 36, 2), A.add, ("sl1",), ("n18",))
-        tt(T.val[:, 0:C], T.dg[:, 0:72].indirect(T.vl[:, 0:18]), v("mv"), A.mult, ("dg", "vl", "mv"), ("val",))
+        tt(T.dg[:, 0:72], v("ra"), v("rb"), A.subtract, ("ra", "rb"), ("dg",))
         ts(v("h18"), v("n18"), 7, A.bitwise_and, R=("n18",), W=("h18",))
         ts(v("w1"), v("n18"), 0.125, A.mult, R=("n18",), W=("w1",))
         ts(v("v1"), v("h18"), 287.875, A.mult, R=("h18",), W=("v1",))
         tt(v("e1"), v("v1"), v("w1"), A.add, ("v1", "w1"), ("e1",))
+        tt(T.val[:, 0:C], T.dg[:, 0:72].indirect(T.vl[:, 0:18]), v("mv"), A.mult, ("dg", "vl", "mv"), ("val",))
         cp(T.sl[:, 0:18], v("e1"), ("e1",), ("sl",))
         if r == 0:
             quant("scq", 576, 704, T.scw[:, 2304:2816], ("scw",), ("scqp",))
         cp(T.scw[:, 0:2304].indirect(T.sl[:, 0:18]), T.val[:, 0:C], ("sl", "val"), ("scw",))
+        if r == 0:
+            for b in range(4):
+                a = 4 * (112 + 4 * b) + b
+                op("v", lambda a=a: g.vector.memset(v("clz", a, a + 13, 4), 2.0), (), ("clz",))
+            quant("lzq", 0, 240, v("clz"), ("clz",), ("lzq",))
         for k in range(2):
             quant("scq", 288 * k, 288 * k + 288, T.scw[:, 1152 * k:1152 * k + 1152], ("scw",), ("scq%d" % k,))
         for h in range(8):
             a = 72 * h
             R = ["lzq"] + (["scq0"] if a < 288 else []) + (["scq1"] if a + 128 > 288 else []) + (["scqp"] if a + 128 > 576 else [])
-            mm(0, 128, "lzq", 112 - 16 * h, "scq", a, R, h == 0, h == 7)
-        tt(v("yi"), v("yc"), ps(0, 72), A.add, ("yc",), ("yi",), (0,))
-        ts(v("si"), v("yi"), 7, A.bitwise_and, R=("yi",), W=("si",))
-        ts(v("o1"), v("yi"), 0.5, A.mult, cA, A.add, R=("yi", "cf"), W=("o1",))
-        ts(v("o2"), v("si"), TB - 0.5, A.mult, R=("si",), W=("o2",))
-        tt(v("o3"), v("o1"), v("o2"), A.add, ("o1", "o2"), ("o3",))
-        cp(T.off[:, 0:72], v("o3"), ("o3",), ("off",))
-        win = t0 + edges + ["twr"]
+            mm(1, 128, "lzq", 112 - 16 * h, "scq", a, R, h == 0, h == 7)
+        tt(v("ni"), v("yc"), ps(1, 72), A.add, ("yc",), ("ni",), (1,))
+        offsets("off")
+        win = t0 + ["twr"] + ["tw%d%d" % (s, b) for s in range(1 + BYDMA[r], 8) for b in range(4)]
         cp(T.gt[:, 0:576], T.tw[:, 0:8 * TB].indirect(T.off[:, 36:72]), win + ["off"], ("gt",))
         quant("gq", 0, H, T.gt[:, 0:576], ("gt",), ("gq",))
         send(dst, "ga%d" % r, "sg%d" % r, "gq", "lg%d" % r)
         cp(T.ft[:, 0:576], T.tw[:, 0:8 * TB].indirect(T.off[:, 0:36]), win + ["off"], ("ft",))
         quant("fq", 0, H, T.ft[:, 0:576], ("ft",), ("fq",))
         layer("fq", "at", False)
-        ts(v("yn"), v("nn"), v("cx", 0, 1), A.add, R=("nn", "cx0"), W=("yn",))
         cp(v("ni"), v("nn"), ("nn",), ("ni",))
-        ts(v("sn"), v("yn"), 7, A.bitwise_and, R=("yn",), W=("sn",))
-        ts(v("cn"), v("ni"), 3, A.arith_shift_right, R=("ni",), W=("cn",))
-        ts(v("p1"), v("sn"), 1152.0, A.mult, R=("sn",), W=("p1",))
-        ts(v("p2"), v("cn"), 4.0, A.mult, cA, A.add, R=("cn", "cf"), W=("p2",))
-        tt(v("p3"), v("p1"), v("p2"), A.add, ("p1", "p2"), ("p3",))
-        cp(T.off2[:, 0:72], v("p3"), ("p3",), ("off2",))
+        offsets("off2")
         quant("aq", 0, H, T.at[:, 0:576], ["at%d" % b for b in range(4)], ("aq",))
-        if r == 0:
-            quant("vq", 0, 128, T.vt[:, 0:512], ("vt",), ("vq",))
+        unpack("aq", 0, "va", 0, 4)
+        dma("y", "ta%d" % r, turned(T.vw, 0, 576, range(1, 8)), va, ("vat",))
         layer("lg%d" % r, "bt", True)
         quant("bq", 0, H, T.bt[:, 0:576], ["bt%d" % b for b in range(4)], ("bq",))
         send(dst, "bl%d" % r, "sb%d" % r, "bq", "lb%d" % r)
         if r < 2:
-            op("g", lambda: g.iota(T.scw[:, 0:2304], [[0, 2304]], 0, 0, allow_small_or_imprecise_dtypes=True), (), ("scw",))
-        unpack("aq", 0, "va")
-        if r == 2:
+            iota(T.scw[:, 0:2304], [[0, 2304]], "scw")
+        if r == 1:
             for b in range(1, 4):
                 act(T.fe2[:, b:4 * C:4], v("zf"), F.Copy, ("zf",), ("fe2%d" % b,))
+            act(v("pc"), v("rp"), F.Identity, ("rp", "cx16"), ("pc",), bias=col(16))
+            quant("vq", 0, 128, T.vt[:, 0:512], ("vt",), ("vq",))
+        if r == 2:
             act(T.fe2[:, 0:4 * C:4], T.fe[:, 0:C], F.Copy, ("fe",), ("fe20",))
             quant("f2q", 0, C, T.fe2[:, 0:4 * C], ["fe2%d" % b for b in range(4)], ("f2q",))
             mm(0, C, "s1q", 0, "f2q", 0, ("s1q", "f2q"))
             mm(1, C, "s2q", 0, "f2q", 0, ("s2q", "f2q"))
             scan(v("cr"), ps(0, C), C, (), ("cr",), (0,))
             tt(v("xr"), v("cr"), ps(1, C), A.subtract, ("cr",), ("xr",), (1,))
-            ts(v("pc"), v("rp"), v("cx", 16, 17), A.add, R=("rp", "cx16"), W=("pc",))
-            ts(v("yr"), v("xr"), 2.0, A.mult, -1152.0, A.add, R=("xr",), W=("yr",))
+            act(v("yr"), v("xr"), F.Identity, ("xr",), ("yr",), scale=2.0, bias=-1152.0)
             tt(v("zr"), v("yr"), T.fe[:, 0:C], A.mult, ("yr", "fe"), ("zr",))
             tt(v("nr"), v("zr"), v("pc"), A.add, ("zr", "pc"), ("nr",))
             buf, at, w = _SHARE["nr"]
             dma("y", "oo", [(T.op[k:k + 1, 0:C], T[buf][16 * k:16 * k + 1, at:at + C]) for k in range(8)], ("nr",), ())
-        unpack("lb%d" % r, 576, "vb")
-        tt(T.xt[:, 0:4 * C], T.vw[:, 0:8 * 4 * C].indirect(T.off2[:, 0:72]), T.tw[:, 4:1156], A.add,
-           ["va%d" % k for k in range(32)] + ["vb%d" % k for k in range(32)] + ["off2"] + t0, ("xt",))
+        vb = ["vb%d" % k for k in range(4 * BDMA)]
+        unpack("lb%d" % r, 576, "vb", 0, 4)
+        dma("y", "tb%d" % r, turned(T.vw, 576, 576, range(BDMA, 8)), vb[:4], ("vbt",))
+        unpack("lb%d" % r, 576, "vb", 4, 4 * BDMA)
+        tt(T.xt[:, 0:4 * C], T.vw[:, 0:8 * TB].indirect(T.off2[:, 0:72]), T.tw[:, 0:TB], A.add,
+           va + vb + ["vat", "vbt", "off2"] + t0, ("xt",))
 
     quant("q", 0, C, T.xt[:, 0:4 * C], ("xt",), ("q",))
     mm(0, C, "vq", 0, "q", 0, ("vq", "q"))

from concourse.mybir import dt, AluOpType, AxisListType, ActivationFunctionType

MASK = [4, 1, 2]
C, H = 288, 144
NV = 8
TB = 4 * C
BYDMA = [7, 6, 6]
BDMA = 6
F8, U8, BF, F32, I32, U16 = "float8_e4m3fn_x4", "uint8", "bfloat16", "float32", "int32", "uint16"

SCRATCH = {}
_SHARE = {}


def _add(dtype, *sizes):
    for n, w in sizes:
        SCRATCH[n] = ("sbuf", [128, w], dtype)


def _mx(*sizes):
    for n, w in sizes:
        SCRATCH[n] = ("sbuf", [128, w], F8)
        SCRATCH[n + "s"] = ("sbuf", [128, w], U8)


def _pack(into, dtype, *sizes):
    at = 0
    for n, w in sizes:
        _SHARE[n] = (into, at, w)
        at += (w + 7) // 8 * 8
    SCRATCH[into] = ("sbuf", [128, at], dtype)


_mx(("q", C), ("uq", 128), ("urq", 128), ("vq", 128), ("wq", 512), ("gq", H), ("fq", H), ("aq", H), ("bq", H), ("nq", 128),
    ("scq", 704), ("f2q", C), ("gaq", 128), ("gbq", 128), ("s1q", 128), ("s2q", 128), ("s3q", 128), ("s4q", 128), ("lzq", 240))
_mx(*[("flq%d" % k, C) for k in range(5)], *[("idq%d" % k, 256) for k in range(4)])
_mx(*[("%s%d" % (n, k), H) for n in ("lg", "lb") for k in range(3)])
_add(BF, *[("fl%d" % k, 4 * C) for k in range(5)])
_add(BF, ("xt", 4 * C), ("ut", 512), ("vt", 512), ("gt", 4 * H), ("ft", 4 * H), ("at", 4 * H), ("bt", 4 * H), ("tw", 8 * TB),
     ("vw", 8 * TB), ("scw", 2816), ("fe", 512), ("fe2", 4 * C), ("wk", 1032), ("val", C), ("junk", C))
_pack("ctile", BF, ("cga", 512), ("cgb", 512), ("cs1", 512), ("cs2", 512), ("cs3", 512), ("cs4", 512), ("clz", 960))
_pack("rows", F32, ("zf", C), ("r256", 256), ("r16", C), ("rg4", 512), ("rr", 128), ("rv", C), ("rs", 72), ("rt", 72), ("ry", 72),
      ("r4c", 18), ("rp", C), ("m0", C))
_pack("cons", F32, ("cf", 8), ("cx", 40), ("mo", C), ("mv", C), ("ms", 72), ("nc", 72), ("yc", 72), ("pc", C))
_pack("temp", F32, ("mm", C), ("n1", C), ("m1", C), ("ec", C), ("hs", C), ("key", C),
      ("sm", 32), ("cc", 72), ("xx", 72), ("zz", 72), ("t2", 72), ("nn", 72), ("ra", 72), ("rb", 72), ("sl0", 72), ("sl1", 36),
      ("v1", 18), ("w1", 18), ("e1", 18), ("o1", 72), ("o2", 72), ("o3", 72), ("nr", C),
      ("cr", C), ("xr", C), ("yr", C), ("zr", C))
_pack("ints", I32, ("ci", 8), ("ru", 8), ("n18", 18), ("h18", 18), ("yi", 72), ("si", 72), ("ji", 72), ("ni", 72))
_add(F32, ("ow", C), ("dg", 72), ("yo", C))
_add(U16, ("ul", 8), ("vl", 18), ("sl", 18), ("off", 72), ("off2", 72))
SCRATCH["ps"] = ("psum", [128, 4096], F32)

SEMAPHORES = (["qv", "qs", "qp", "qg", "dx", "du", "dv", "dw", "oy", "oo", "oq"]
              + ["%s%d" % (n, r) for n in ("tr", "ta", "tb", "ga", "bl", "sg", "sb") for r in range(3)])


def rank_program(g, core, T, topo):
    rank = T.rank_of(core)
    if rank is None:
        return
    A, F, X = AluOpType, ActivationFunctionType, AxisListType
    queue = {"v": g.vector, "s": g.scalar, "p": g.tensor, "g": g, "y": g.sync}
    total, seen, last, banks = {}, {}, {}, {}

    def v(name, a=0, b=None, st=1):
        buf, at, w = _SHARE[name] if name in _SHARE else (name, 0, SCRATCH[name][1][1])
        b = w if b is None else b
        return T[buf][:, at + a:at + b] if st == 1 else T[buf][:, at + a:at + b:st]

    def before(q, R, W, B):
        deps = {}
        toks = [t for k in R for t in last.get(k, ([], []))[0]]
        toks += [t for k in W for half in last.get(k, ([], [])) for t in half]
        toks += [t for b in B for qq, t in banks.get(b, {}).items() if qq != q]
        for s, n in toks:
            deps[s] = max(deps.get(s, 0), n)
        for s, n in deps.items():
            if seen.get((q, s), 0) < n:
                queue[q].wait_ge(T.sem[s], n)
                seen[(q, s)] = n

    def after(q, R, W, B, tok):
        for k in R:
            last.setdefault(k, ([], []))[1].append(tok)
        for k in W:
            last[k] = ([tok], [])
        for b in B:
            banks.setdefault(b, {})[q] = tok

    def op(q, call, R=(), W=(), B=()):
        before(q, R, W, B)
        s = "q" + q
        call().then_inc(T.sem[s], 1)
        total[s] = total.get(s, 0) + 1
        after(q, R, W, B, (s, total[s]))

    def dma(q, s, pairs, R=(), W=()):
        before(q, R, W, ())
        for o, i in pairs:
            queue[q].dma_start(o, i).then_inc(T.sem[s], 16)
            total[s] = total.get(s, 0) + 16
        after(q, R, W, (), (s, total[s]))

    def ts(o, i, s1, o1, s2=None, o2=None, R=(), W=(), B=()):
        if o2 is None:
            op("v", lambda: g.vector.tensor_scalar(o, i, s1, None, o1), R, W, B)
        else:
            op("v", lambda: g.vector.tensor_scalar(o, i, s1, s2, o1, o2), R, W, B)

    def tt(o, a, b, o1, R=(), W=(), B=()):
        op("v", lambda: g.vector.tensor_tensor(o, a, b, o1), R, W, B)

    def cp(o, i, R=(), W=(), B=()):
        op("v", lambda: g.vector.tensor_copy(o, i), R, W, B)

    def scan(o, i, n, R=(), W=(), B=()):
        op("v", lambda: g.vector.tensor_tensor_scan(o, i, v("zf", 0, n), 0.0, A.add, A.add), tuple(R) + ("zf",), W, B)

    def act(o, i, f, R=(), W=(), B=(), **k):
        op("s", lambda: g.scalar.activation(o, i, f, **k), R, W, B)

    def quant(name, a, b, tile, R, W):
        op("v", lambda: g.vector.quantize_mx(v(name, a, b), v(name + "s", a, b), tile), R, W)

    def ps(bank, n):
        return T.ps[:, 512 * bank:512 * bank + n]

    def mm(bank, n, l, la, r, ra, R, start=True, stop=True):
        op("p", lambda: g.tensor.matmul_mx(ps(bank, n), v(l, la, la + 128), v(l + "s", la, la + 128),
                                           v(r, ra, ra + n), v(r + "s", ra, ra + n), start, stop), R, (), (bank,))

    def iota(o, pattern, key, base=0, cm=0, whole=False):
        if whole:
            op("g", lambda: g.iota(o, pattern, base, cm), (), (key,))
        else:
            op("g", lambda: g.iota(o, pattern, base, cm, allow_small_or_imprecise_dtypes=True), (), (key,))

    def row(name, pattern, base=0):
        iota(v(name), pattern, name, base)

    def turned(win, at, n, rots):
        out = []
        for s in rots:
            k, a = 128 - 16 * s, TB * s + at
            out.append((win[0:k, a:a + n], win[16 * s:128, at:at + n]))
            out.append((win[k:128, a:a + n], win[0:16 * s, at:at + n]))
        return out

    dma("y", "du", [(T.ut[:, :], T.u[:, :])], (), ("ut",))
    dma("y", "dx", [(T.xt[:, :], T.x[:, :])], (), ("xt",))
    iota(v("ci", 0, 1), [[1, 1]], "ci", 0, 1, True)
    iota(v("ru"), [[16, 8]], "ru", 0, 0, True)
    row("r256", [[0, 2], [1, 128]])
    row("rr", [[1, 8], [8, 4], [0, 4]])
    row("r16", [[0, 18], [1, 16]])
    row("rg4", [[1, 8], [0, 64]])
    row("zf", [[0, C]])
    iota(T.fe[:, 288:512], [[0, 224]], "fez")
    row("rt", [[16, 72]], 576)
    row("ry", [[0, 2], [64, 36]])
    row("r4c", [[4, 18]])
    row("rv", [[0, 18], [1, 4], [0, 4]])
    row("rs", [[0, 18], [1, 4]])
    row("clz", [[0, 960]])
    row("scw", [[0, 2816]])
    row("rp", [[4, C]], 576)

    op("v", lambda: g.vector.memset(v("wk"), 0.0), (), ("wk",))
    ts(v("ci", 2, 3), v("ci", 0, 1), 4, A.arith_shift_right, R=("ci",), W=("ci2",))
    ts(v("ci", 1, 2), v("ci", 0, 1), 15, A.bitwise_and, R=("ci",), W=("ci1",))
    ts(v("ci", 3, 4), v("ci", 0, 1), 2, A.arith_shift_right, 3, A.bitwise_and, R=("ci",), W=("ci3",))
    ts(v("ci", 4, 5), v("ci", 0, 1), 3, A.bitwise_and, R=("ci",), W=("ci4",))
    cp(v("cf", 0, 5), v("ci", 0, 5), ("ci", "ci1", "ci2", "ci3", "ci4"), ("cf",))
    cP, cI, cG, cR, cA = [v("cf", k, k + 1) for k in range(5)]
    cp(v("ul"), v("ru"), ("ru",), ("ul",))
    ts(v("wk", 3, 1024, 4), v("r256"), cP, A.is_equal, R=("r256", "cf"), W=("wk",))
    for b in range(4):
        quant("idq%d" % b, 0, 256, v("wk", 3 - b, 1027 - b), ("wk",), ("idq%d" % b,))
    quant("uq", 0, 128, T.ut[:, 0:512], ("ut",), ("uq",))
    cp(T.urq[:, 0:128].bitcast(dt.uint32), T.uq[:, 0:128].bitcast(dt.uint32).indirect(T.ul[:, 0:8]), ("uq", "ul"), ("urq",))
    cp(T.urqs[:, 0:128], T.uqs[:, 0:128].indirect(T.ul[:, 0:8]), ("uq", "ul"), ("urqs",))
    ts(v("mo"), v("r16"), cI, A.is_equal, R=("r16", "cf"), W=("mo",))

    def col(k):
        return v("cx", k, k + 1)

    def ccol(k, i, f, R, **kw):
        act(col(k), i, f, R, ("cx%d" % k,), **kw)

    c2, c3 = ["cs2%d" % b for b in range(4)], ["cs3%d" % b for b in range(4)]
    for b in range(4):
        ccol(5 + b, cG, F.Identity, ("cf",), bias=8.0 * b + 0.5)
        ccol(22 + b, cG, F.Identity, ("cf",), bias=8.0 * b)
    for b in range(4):
        act(v("cs2", b, 512, 4), v("rr"), F.Sign, ("rr", "cx%d" % (5 + b)), (c2[b],), scale=-1.0, bias=col(5 + b))
        act(v("cs3", b, 512, 4), v("rr"), F.Abs, ("rr", "cx%d" % (22 + b)), (c3[b],), scale=-1.0, bias=col(22 + b))
    act(v("cs2"), v("cs2"), F.Identity, c2, ("cs2",), scale=0.03125, bias=0.03125)
    act(v("cs3"), v("cs3"), F.Relu, c3, ("cs3",), scale=-1.0, bias=1.0)
    act(v("m0"), v("r16"), F.Sign, ("r16",), ("m0",))
    for b in (2, 3):
        act(T.fl4[:, b:4 * C:4], v("zf"), F.Copy, ("zf",), ("fl4%d" % b,))
    t0, va = ["tw0%d" % b for b in range(4)], ["va%d" % k for k in range(4)]

    def more_constants():
        act(v("cs4"), v("cs3"), F.Copy, ("cs3",), ("cs4",), scale=72.0)
        act(v("cs3"), v("cs3"), F.Copy, ("cs3",), ("cs3",), scale=-0.125)
        ccol(1, cR, F.Copy, ("cf",), scale=4.0)
        ccol(3, cR, F.Copy, ("cf",), scale=16.0)
        for k in range(3):
            ccol(26 + k, cA, F.Identity, ("cf",), bias=-0.5 - k)
        ccol(2, cG, F.Identity, ("cf", "cx1"), scale=0.5, bias=col(1))
        ccol(4, cG, F.Identity, ("cf", "cx3"), scale=2.0, bias=col(3))
        for k in range(3):
            ccol(9 + k, col(26 + k), F.Sign, ("cx%d" % (26 + k),))
        act(v("nc"), v("rt"), F.Identity, ("rt", "cx2"), ("nc",), bias=col(2))
        act(v("yc"), v("ry"), F.Identity, ("ry", "cx4"), ("yc",), bias=col(4))
        for k in range(3):
            ccol(17 + k, col(9 + k), F.Identity, ("cx%d" % (9 + k),), scale=7.5, bias=8.5)
        ccol(12, col(17), F.Copy, ("cx17",), scale=1.5 * 2.0 ** 22)
        ccol(13, col(18), F.Copy, ("cx18", "cx12"), scale=col(12))
        ccol(14, col(19), F.Copy, ("cx19", "cx13"), scale=col(13))
        ccol(15, col(14), F.Copy, ("cx14",), scale=16.0)
        ccol(20, col(14), F.Copy, ("cx14",), scale=-1.0)
        ccol(21, col(14), F.Copy, ("cx14",), scale=-16.0)
        ccol(0, cG, F.Identity, ("cf",), scale=-1.0, bias=8.0)
        ccol(16, cG, F.Copy, ("cf",), scale=0.5)

    def send(dst, arrive, left, src, land):
        both = topo.mask(core, dst) & topo.mask(core, T.cores[rank ^ MASK[0]])
        ne = bin(both).count("1")
        rid, pid = topo.addr(dst, core)
        before("g", (src,), (), ())
        g.remote_dma(T[land][:, 0:H].bitcast(dt.uint8), T[src][:, 0:H].bitcast(dt.uint8), T.sem[arrive], T.sem[left], pid, rid, both)
        g.remote_dma(T[land + "s"][:, 0:H], T[src + "s"][:, 0:H], T.sem[arrive], T.sem[left], pid, rid, both)
        total[left] = total[arrive] = 2 * ne
        after("g", (src,), (), (), (left, 2 * ne))
        last[land] = ([(arrive, 2 * ne)], [])

    def layer(code, tile, split):
        for b in range(4):
            q = "s" if not split or b % 2 else "v"
            bank = (4 + b) if q == "s" else b
            mm(bank, H, "wq", 128 * b, code, 0, ("wq", code))
            o = T[tile][:, b:4 * H:4]
            if q == "s":
                act(o, ps(bank, H), F.Relu, (), (tile + str(b),), (bank,), scale=0.03125)
            else:
                ts(o, ps(bank, H), 0.0, A.max, 0.03125, A.mult, W=(tile + str(b),), B=(bank,))

    def unpack(code, base, tag, lo, hi):
        for k in range(lo, hi):
            s, b = k // 4, k % 4
            q = "vs"[k % 2]
            bank = (k // 2) % 4 + (4 if q == "s" else 0)
            mm(bank, H, "idq%d" % b, 16 * s, code, 0, ("idq%d" % b, code))
            o = T.vw[:, TB * s + base + b:TB * s + base + 576:4]
            if q == "s":
                act(o, ps(bank, H), F.Copy, (), ("%s%d" % (tag, k),), (bank,))
            else:
                cp(o, ps(bank, H), (), ("%s%d" % (tag, k),), (bank,))

    def turn(r, lo, hi):
        for k in range(lo, min(hi, 4 * (7 - BYDMA[r]))):
            s, b = 1 + BYDMA[r] + k // 4, k % 4
            mm(4 + k % 3, C, "idq%d" % b, 16 * s, "q", 0, ("idq%d" % b, "q"))
            act(T.tw[:, TB * s + b:TB * s + TB:4], ps(4 + k % 3, C), F.Copy, (), ("tw%d%d" % (s, b),), (4 + k % 3,))

    def offsets(out):
        ts(v("yi"), v("ni"), col(0), A.add, R=("ni", "cx0"), W=("yi",))
        ts(v("ji"), v("ni"), 3, A.arith_shift_right, R=("ni",), W=("ji",))
        ts(v("si"), v("yi"), 7, A.bitwise_and, R=("yi",), W=("si",))
        ts(v("o1"), v("ji"), 4.0, A.mult, cA, A.add, R=("ji", "cf"), W=("o1",))
        ts(v("o2"), v("si"), float(TB), A.mult, R=("si",), W=("o2",))
        tt(v("o3"), v("o1"), v("o2"), A.add, ("o1", "o2"), ("o3",))
        cp(T[out][:, 0:72], v("o3"), ("o3",), (out,))

    def sm(k):
        return v("sm", k, k + 1)

    for r in range(3):
        dst = T.cores[rank ^ MASK[r]]
        quant("q", 0, C, T.xt[:, 0:4 * C], ("xt",), ("q",))
        for bank in (0, 4):
            mm(bank, C, "urq", 0, "q", 0, ("urq", "urqs", "q"))
        for b, bank in enumerate((2, 3, 5, 7)):
            mm(bank, C, "idq%d" % b, 0, "q", 0, ("idq%d" % b, "q"))
            act(T.tw[:, b:TB:4], ps(bank, C), F.Copy, (), ("tw0%d" % b,), (bank,))
        dma("y", "tr%d" % r, turned(T.tw, 0, TB, range(1, 1 + BYDMA[r])), t0, ("twr",))
        if r == 0:
            dma("y", "dw", [(T.wq[:, :].bitcast(dt.uint8), T.wc[:, :]), (T.wqs[:, :], T.ws[:, :])], (), ("wq",))
            dma("y", "dv", [(T.vt[:, :], T.v[:, :])], (), ("vt",))
            ts(v("cgb"), v("rg4"), cG, A.is_equal, R=("rg4", "cf"), W=("cgb",))
            ts(v("cga"), v("cgb"), 2.0, A.mult, R=("cgb",), W=("cga",))
        tt(v("mm"), ps(0, C), v("mo"), A.mult, ("mo",), ("mm",), (0,))
        op("v", lambda: g.vector.tensor_tensor_scan(v("ow"), v("m0"), v("mm"), 0.0, A.mult, A.add), ("m0", "mm"), ("ow",))
        for t in range(NV, 18):
            k = t // 4
            act(T["fl%d" % k][:, t % 4:4 * C:4], ps(4, C), F.Sign, ("ow",), ("fl%d%d" % (k, t % 4),), (4,),
                scale=-1.0, bias=v("ow", 16 * t + 15, 16 * t + 16))
        for k in range(5):
            if k < 2:
                for b in range(4):
                    a = 16 * (4 * k + b) + 15
                    ts(T["fl%d" % k][:, b:4 * C:4], ps(0, C), v("ow", a, a + 1), A.is_lt, R=("ow",), W=("fl%d%d" % (k, b),), B=(0,))
            if r == 0 and k == 0:
                quant("gaq", 0, 128, v("cga"), ("cga",), ("gaq",))
                quant("gbq", 0, 128, v("cgb"), ("cgb",), ("gbq",))
            quant("flq%d" % k, 0, C, T["fl%d" % k][:, 0:4 * C], ["fl%d%d" % (k, b) for b in range(4)], ("flq%d" % k,))
            for bank in (1, 6):
                w = "gaq" if k < 2 else "gbq"
                mm(bank, C, w, 0, "flq%d" % k, 0, (w, "flq%d" % k), k == 0, k == 4)
        act(v("junk"), ps(6, C), F.Sign, (), ("junk", "sm0"), (6,), scale=-1.0, bias=127.5, accum_out=sm(0))
        act(sm(10), sm(0), F.Sign, ("sm0",), ("sm10",), bias=0.5)
        act(sm(6), sm(0), F.Identity, ("sm0",), ("sm6",), scale=-1.0 / 2048, bias=2048.0 + 1.0 / 2048)
        act(sm(3), sm(10), F.Relu, ("sm10",), ("sm3",))
        act(sm(7), sm(3), F.Identity, ("sm3", "sm6"), ("sm7",), scale=-2048.0, bias=sm(6))
        if r == 0:
            more_constants()
        turn(r, 0, 28)
        ts(v("n1"), ps(1, C), 128.0, A.is_ge, -2048.0, A.mult, W=("n1",), B=(1,))
        tt(v("m1"), ps(1, C), v("n1"), A.add, ("n1",), ("m1",), (1,))
        op("v", lambda: g.vector.tensor_reduce(sm(1), v("m1"), X.X, A.max), ("m1",), ("sm1",))
        op("v", lambda: g.vector.tensor_reduce(sm(2), v("m1"), X.X, A.min), ("m1",), ("sm2",))
        tt(sm(4), sm(1), sm(2), A.subtract, ("sm1", "sm2"), ("sm4",))
        ts(sm(5), sm(4), sm(3), A.mult, sm(2), A.add, R=("sm4", "sm3", "sm2"), W=("sm5",))
        ts(v("ec"), v("m1"), sm(5), A.is_equal, 1.0 / 1024, A.mult, R=("m1", "sm5"), W=("ec",))
        tt(sm(8), sm(7), sm(5), A.add, ("sm7", "sm5"), ("sm8",))
        scan(v("hs"), v("ec"), C, ("ec",), ("hs",))
        ts(sm(9), v("hs", 287, 288), sm(3), A.mult, sm(8), A.add, R=("hs", "sm3", "sm8"), W=("sm9",))
        tt(v("key"), ps(1, C), v("hs"), A.add, ("hs",), ("key",), (1,))
        ts(T.fe[:, 0:C], v("key"), sm(9), A.is_lt, 0.5, A.subtract, R=("key", "sm9"), W=("fe",))
        quant("nq", 0, 128, T.fe[:, 0:512], ("fe", "fez"), ("nq",))
        if r == 0:
            op("v", lambda: g.vector.memset(v("cs1"), 0.0625), (), ("cs1",))
            for k in range(1, 5):
                quant("s%dq" % k, 0, 128, v("cs%d" % k), ("cs%d" % k,), ("s%dq" % k,))
        for bank, w in ((2, "s1q"), (3, "s2q"), (0, "s3q"), (7, "s4q")):
            mm(bank, 128, w, 0, "nq", 0, (w, "nq"))
        scan(v("cc"), ps(2, 72), 72, (), ("cc",), (2,))
        tt(v("xx"), v("cc"), ps(3, 72), A.subtract, ("cc",), ("xx",), (3,))
        tt(v("zz"), v("xx"), ps(0, 72), A.mult, ("xx",), ("zz",), (0,))
        act(v("rb"), v("zz"), F.Identity, ("zz", "cx15"), ("rb",), bias=col(15))
        act(v("ra"), v("zz"), F.Identity, ("zz", "cx14"), ("ra",), bias=col(14))
        act(v("rb"), v("rb"), F.Identity, ("rb", "cx21"), ("rb",), bias=col(21))
        act(v("ra"), v("ra"), F.Identity, ("ra", "cx20"), ("ra",), bias=col(20))
        if r == 0:
            ts(v("ms"), v("rs"), cA, A.is_equal, R=("rs", "cf"), W=("ms",))
        tt(v("t2"), v("zz"), ps(7, 72), A.add, ("zz",), ("t2",), (7,))
        tt(v("nn"), v("nc"), v("t2"), A.subtract, ("nc", "t2"), ("nn",))
        tt(v("sl0"), v("nn"), v("ms"), A.mult, ("nn", "ms"), ("sl0",))
        tt(v("sl1"), v("sl0", 0, 72, 2), v("sl0", 1, 72, 2), A.add, ("sl0",), ("sl1",))
        if r == 0:
            ts(v("mv"), v("rv"), cR, A.is_equal, R=("rv", "cf"), W=("mv",))
            ts(v("vl"), v("r4c"), cA, A.add, R=("r4c", "cf"), W=("vl",))
        tt(v("n18"), v("sl1", 0, 36, 2), v("sl1", 1, 36, 2), A.add, ("sl1",), ("n18",))
        tt(T.dg[:, 0:72], v("ra"), v("rb"), A.subtract, ("ra", "rb"), ("dg",))
        ts(v("h18"), v("n18"), 7, A.bitwise_and, R=("n18",), W=("h18",))
        ts(v("w1"), v("n18"), 0.125, A.mult, R=("n18",), W=("w1",))
        ts(v("v1"), v("h18"), 287.875, A.mult, R=("h18",), W=("v1",))
        tt(v("e1"), v("v1"), v("w1"), A.add, ("v1", "w1"), ("e1",))
        tt(T.val[:, 0:C], T.dg[:, 0:72].indirect(T.vl[:, 0:18]), v("mv"), A.mult, ("dg", "vl", "mv"), ("val",))
        cp(T.sl[:, 0:18], v("e1"), ("e1",), ("sl",))
        if r == 0:
            quant("scq", 576, 704, T.scw[:, 2304:2816], ("scw",), ("scqp",))
        cp(T.scw[:, 0:2304].indirect(T.sl[:, 0:18]), T.val[:, 0:C], ("sl", "val"), ("scw",))
        if r == 0:
            for b in range(4):
                a = 4 * (112 + 4 * b) + b
                op("v", lambda a=a: g.vector.memset(v("clz", a, a + 13, 4), 2.0), (), ("clz",))
            quant("lzq", 0, 240, v("clz"), ("clz",), ("lzq",))
        for k in range(2):
            quant("scq", 288 * k, 288 * k + 288, T.scw[:, 1152 * k:1152 * k + 1152], ("scw",), ("scq%d" % k,))
        for h in range(8):
            a = 72 * h
            R = ["lzq"] + (["scq0"] if a < 288 else []) + (["scq1"] if a + 128 > 288 else []) + (["scqp"] if a + 128 > 576 else [])
            mm(1, 128, "lzq", 112 - 16 * h, "scq", a, R, h == 0, h == 7)
        tt(v("ni"), v("yc"), ps(1, 72), A.add, ("yc",), ("ni",), (1,))
        offsets("off")
        win = t0 + ["twr"] + ["tw%d%d" % (s, b) for s in range(1 + BYDMA[r], 8) for b in range(4)]
        cp(T.gt[:, 0:576], T.tw[:, 0:8 * TB].indirect(T.off[:, 36:72]), win + ["off"], ("gt",))
        quant("gq", 0, H, T.gt[:, 0:576], ("gt",), ("gq",))
        send(dst, "ga%d" % r, "sg%d" % r, "gq", "lg%d" % r)
        cp(T.ft[:, 0:576], T.tw[:, 0:8 * TB].indirect(T.off[:, 0:36]), win + ["off"], ("ft",))
        quant("fq", 0, H, T.ft[:, 0:576], ("ft",), ("fq",))
        layer("fq", "at", False)
        cp(v("ni"), v("nn"), ("nn",), ("ni",))
        offsets("off2")
        quant("aq", 0, H, T.at[:, 0:576], ["at%d" % b for b in range(4)], ("aq",))
        unpack("aq", 0, "va", 0, 4)
        dma("y", "ta%d" % r, turned(T.vw, 0, 576, range(1, 8)), va, ("vat",))
        layer("lg%d" % r, "bt", True)
        quant("bq", 0, H, T.bt[:, 0:576], ["bt%d" % b for b in range(4)], ("bq",))
        send(dst, "bl%d" % r, "sb%d" % r, "bq", "lb%d" % r)
        if r < 2:
            iota(T.scw[:, 0:2304], [[0, 2304]], "scw")
        if r == 1:
            for b in range(1, 4):
                act(T.fe2[:, b:4 * C:4], v("zf"), F.Copy, ("zf",), ("fe2%d" % b,))
            act(v("pc"), v("rp"), F.Identity, ("rp", "cx16"), ("pc",), bias=col(16))
            quant("vq", 0, 128, T.vt[:, 0:512], ("vt",), ("vq",))
        if r == 2:
            act(T.fe2[:, 0:4 * C:4], T.fe[:, 0:C], F.Copy, ("fe",), ("fe20",))
            quant("f2q", 0, C, T.fe2[:, 0:4 * C], ["fe2%d" % b for b in range(4)], ("f2q",))
            mm(0, C, "s1q", 0, "f2q", 0, ("s1q", "f2q"))
            mm(1, C, "s2q", 0, "f2q", 0, ("s2q", "f2q"))
            scan(v("cr"), ps(0, C), C, (), ("cr",), (0,))
            tt(v("xr"), v("cr"), ps(1, C), A.subtract, ("cr",), ("xr",), (1,))
            act(v("yr"), v("xr"), F.Identity, ("xr",), ("yr",), scale=2.0, bias=-1152.0)
            tt(v("zr"), v("yr"), T.fe[:, 0:C], A.mult, ("yr", "fe"), ("zr",))
            tt(v("nr"), v("zr"), v("pc"), A.add, ("zr", "pc"), ("nr",))
            buf, at, w = _SHARE["nr"]
            dma("y", "oo", [(T.op[k:k + 1, 0:C], T[buf][16 * k:16 * k + 1, at:at + C]) for k in range(8)], ("nr",), ())
        vb = ["vb%d" % k for k in range(4 * BDMA)]
        unpack("lb%d" % r, 576, "vb", 0, 4)
        dma("y", "tb%d" % r, turned(T.vw, 576, 576, range(BDMA, 8)), vb[:4], ("vbt",))
        unpack("lb%d" % r, 576, "vb", 4, 4 * BDMA)
        tt(T.xt[:, 0:4 * C], T.vw[:, 0:8 * TB].indirect(T.off2[:, 0:72]), T.tw[:, 0:TB], A.add,
           va + vb + ["vat", "vbt", "off2"] + t0, ("xt",))

    quant("q", 0, C, T.xt[:, 0:4 * C], ("xt",), ("q",))
    mm(0, C, "vq", 0, "q", 0, ("vq", "q"))
    cp(T.yo[:, 0:C], ps(0, C), (), ("yo",), (0,))
    dma("y", "oq", [(T.oc[:, 0:4 * C], T.q[:, 0:C].bitcast(dt.uint8))]
        + [(T.osc[4 * k:4 * k + 4, 0:C], T.qs[32 * k:32 * k + 4, 0:C]) for k in range(4)], ("q",), ())
    dma("s", "oy", [(T.y[:, 0:C], T.yo[:, 0:C])], ("yo",), ())
    for s, n in total.items():
        if seen.get(("g", s), 0) < n:
            g.wait_ge(T.sem[s], n)
